import numpy as np
import ml_dtypes


def mxq(x, axis, fmt="e4m3"):
    dtype, down = {"e4m3": (ml_dtypes.float8_e4m3fn, 7), "e5m2": (ml_dtypes.float8_e5m2, 14)}[fmt]
    v = np.moveaxis(np.asarray(x, np.float32).astype(ml_dtypes.bfloat16).astype(np.float64), axis, -1)
    blocks = v.reshape(v.shape[:-1] + (-1, 32))
    amax = np.abs(blocks).max(-1, keepdims=True)
    byte = np.maximum(np.where(amax > 0, np.frexp(amax)[1] - 1 + 127, 0) - down, 1)
    scale = np.exp2(byte - 127.0)
    codes = (blocks / scale).astype(np.float32).astype(dtype).astype(np.float64)
    return np.moveaxis((codes * scale).reshape(v.shape), -1, axis)


WIDE = False


def mx_kscale(k):
    if not WIDE:
        return np.ones(k)
    levels = np.array([10, -10, 5, -5, 0])
    if k % 512:
        return np.exp2(np.random.permutation(np.resize(levels, k // 32))).repeat(32)
    a = np.empty((k // 512, 16))
    for p in range(k // 512):
        a[p, :8] = np.random.permutation(np.resize(levels, 8))
        for g in range(8):
            far = levels[np.abs(levels - a[p, g]) >= 10]
            a[p, g + 8] = far[np.random.randint(len(far))]
    return np.exp2(a.ravel()).repeat(32)


BF16 = ml_dtypes.bfloat16


def bf(x):
    return np.asarray(x, np.float32).astype(BF16)


def f64(x):
    return np.asarray(x).astype(np.float64)

def planes(Y):
    n, m = Y.shape
    b = f64(bf(Y)).reshape(n // 32, 32, m)
    amax = np.abs(b).max(1)
    byte = np.clip(np.where(amax > 0, np.frexp(amax)[1] - 1 + 127 - 7, 1), 1, 254)
    codes = (b * np.exp2(127.0 - byte)[:, None, :]).reshape(n, m).astype(np.float32).astype(ml_dtypes.float8_e4m3fn).view(np.uint8)
    words = codes.reshape(n // 512, 128, 4, m).transpose(0, 1, 3, 2)
    return np.ascontiguousarray(words), np.ascontiguousarray(byte.astype(np.uint8).reshape(n // 512, 16, m))


NODES, D, F, O = 1024, 512, 1024, 1536

def setup_inputs():
    n = np.random.standard_normal
    s1 = mx_kscale(D)
    s2 = mx_kscale(F)
    t = mx_kscale(NODES)
    z = n((NODES, D)) * np.sqrt(2.0) / D ** 0.25
    relation = 1.0 + 0.3 * n(D)
    x = n((NODES, F))
    w = n((F, O)) / np.sqrt(F)
    send = np.exp(0.3 * n(NODES)) / NODES ** 0.25
    recv = 1.5 * np.exp(0.2 * n(NODES)) / NODES ** 0.25
    return {
        "z": bf(z * s1[None, :]),
        "relation": bf(relation / (s1 * s1)),
        "x": bf(x * s2[None, :] / t[:, None]),
        "w": bf(w / s2[:, None]),
        "send": bf(send * t),
        "recv": bf(recv),
        "bias": bf(0.3 * n(O)),
        "gain": bf(np.exp(0.8 * n(O))),
    }

def reference(z, relation, x, w, send, recv, bias, gain):
    z, relation, x, w = f64(z), f64(relation), f64(x), f64(w)
    send, recv, bias, gain = f64(send), f64(recv), f64(bias), f64(gain)
    zr = z * relation[None, :]
    P = mxq(zr, 1) @ mxq(z, 1).T
    A = send[:, None] / (1.0 + np.exp(-P))
    V = mxq(x, 1) @ mxq(w, 0)
    S = mxq(A, 0).T @ mxq(V, 0)
    y = gain[None, :] * np.tanh(recv[:, None] * S + bias[None, :])
    Y = y.T
    words, scales = planes(Y)
    return y, words, scales

@@ -1,0 +1,365 @@
+from contextlib import ExitStack
+
+import concourse.mybir as mybir
+from concourse.masks import make_identity
+
+NODES, D, F, O = 1024, 512, 1024, 1536
+FLOPS = 2 * NODES * NODES * D + 2 * NODES * F * O + 2 * NODES * NODES * O
+
+F32 = mybir.dt.float32
+BF16 = mybir.dt.bfloat16
+U32 = mybir.dt.uint32
+I32 = mybir.dt.int32
+U8 = mybir.dt.uint8
+FP8X4 = mybir.dt.float8_e4m3fn_x4
+ACT = mybir.ActivationFunctionType
+ALU = mybir.AluOpType
+
+P = 128
+PACK = 4
+G = P * PACK
+NG = NODES // G
+FG = F // G
+OG = O // G
+
+
+def tile_distmult_sigmoid_neighbour_mix_h3_kernel(tc, z, relation, x, w, send, recv, bias, gain, out_0, out_1, out_2):
+    nc = tc.nc
+    with ExitStack() as ctx:
+        keep = ctx.enter_context(tc.tile_pool(name="keep", bufs=1))
+        work = ctx.enter_context(tc.tile_pool(name="work", bufs=2))
+        psum = ctx.enter_context(tc.psum_pool(name="psum", bufs=8))
+
+        def bank():
+            return psum.tile([P, G], F32, name="bank", tag="bank")
+
+        def mx_pair(name, width):
+            codes = keep.tile([P, width], U32, name=name + "_codes", align_bytes=64)
+            scales = keep.tile([P, width], U8, name=name + "_scales", align_bytes=64)
+            return codes, scales
+
+        def quantize(pair, src):
+            nc.vector.quantize_mx(out=pair[0].bitcast(FP8X4), scales=pair[1], in_=src)
+
+        def mm(out, lhs, rhs, start, stop):
+            nc.tensor.matmul_mx(out=out, lhsT=lhs[0].bitcast(FP8X4), lhsT_scale=lhs[1],
+                                rhs=rhs[0].bitcast(FP8X4), rhs_scale=rhs[1], start=start, stop=stop)
+
+        def cols(pair, lo, n):
+            return pair[0][:, lo:lo + n], pair[1][:, lo:lo + n]
+
+        ctx.enter_context(tc.manual_schedule())
+        ident = keep.tile([P, P], F32, name="ident")
+        make_identity(nc, ident[:])
+
+        rel_sb = keep.tile([P, PACK], BF16, name="rel_sb")
+        send_sb = keep.tile([P, NG, PACK], BF16, name="send_sb")
+        recv_sb = keep.tile([P, NG, PACK], BF16, name="recv_sb")
+        nc.scalar.dma_start(out=rel_sb[:], in_=relation.rearrange("(p t) -> p t", t=PACK))
+        nc.scalar.dma_start(out=send_sb[:], in_=send.rearrange("(g p t) -> p g t", g=NG, t=PACK))
+        nc.scalar.dma_start(out=recv_sb[:], in_=recv.rearrange("(g p t) -> p g t", g=NG, t=PACK))
+
+        z_raw, x_raw, w_raw = {}, {}, {}
+
+        def load_z(g, h):
+            z_raw[g, h] = keep.tile([P, 2 * D], BF16, name="z_raw%d%d" % (g, h))
+            rows = z[g * G:(g + 1) * G, :].rearrange("(m t) d -> m (t d)", t=PACK)
+            nc.sync.dma_start(out=z_raw[g, h][:], in_=rows[:, 2 * h * D:2 * (h + 1) * D])
+
+        def load_x(g, h):
+            x_raw[g, h] = keep.tile([P, 2 * F], BF16, name="x_raw%d%d" % (g, h))
+            rows = x[g * G:(g + 1) * G, :].rearrange("(m t) f -> m (t f)", t=PACK)
+            nc.sync.dma_start(out=x_raw[g, h][:], in_=rows[:, 2 * h * F:2 * (h + 1) * F])
+
+        def load_w(og, c):
+            w_raw[og, c] = work.tile([P, PACK, G], BF16, name="w_raw", tag="w_raw", bufs=4)
+            nc.sync.dma_start(out=w_raw[og, c][:],
+                              in_=w[c * G:(c + 1) * G, og * G:(og + 1) * G].rearrange("(p t) o -> p t o", t=PACK))
+
+        load_z(0, 0)
+        load_w(0, 0)
+        load_z(0, 1)
+        load_z(1, 0)
+        load_z(1, 1)
+        load_x(0, 0)
+        load_x(0, 1)
+        load_w(0, 1)
+        load_x(1, 0)
+        load_x(1, 1)
+        load_w(1, 0)
+        load_w(1, 1)
+        bias_sb = keep.tile([P, O], BF16, name="bias_sb")
+        gain_sb = keep.tile([P, O], BF16, name="gain_sb")
+        nc.sync.dma_start(out=bias_sb[:], in_=bias.partition_broadcast(P))
+        nc.sync.dma_start(out=gain_sb[:], in_=gain.partition_broadcast(P))
+
+        z_mx = [mx_pair("z%d" % g, G) for g in range(NG)]
+        zr_mx = [mx_pair("zr%d" % g, G) for g in range(NG)]
+        x_mx = [mx_pair("x%d" % g, FG * G) for g in range(NG)]
+        w_mx = {(og, c): mx_pair("w%d%d" % (og, c), G) for og in range(OG) for c in range(FG)}
+        a_mx = {(gj, gi): mx_pair("a%d%d" % (gj, gi), G) for gj in range(NG) for gi in range(NG)}
+        v_mx = {(og, gj): mx_pair("v%d%d" % (og, gj), G) for og in range(OG) for gj in range(NG)}
+        y_scales = [keep.tile([P, NODES], U8, name="y_scales%d" % og, align_bytes=64) for og in range(OG)]
+
+        banks = {}
+        zt, zrt, xt, wt, sig, at, vt, pre, yf, ys, yt = {}, {}, {}, {}, {}, {}, {}, {}, {}, {}, {}
+
+        def turn_z(g, h):
+            ps = banks["z", g, h] = bank()
+            words = z_raw[g, h][:].bitcast(F32)
+            for t in range(2):
+                for u in range(2):
+                    q = 2 * t + u
+                    nc.tensor.transpose(ps[:, q * P:(q + 1) * P], words[:, t * 256 + u:(t + 1) * 256:2], ident[:])
+
+        def drain_z(g, h):
+            if h == 0:
+                zt[g] = work.tile([P, G * PACK], BF16, name="zt", tag="zt", align_bytes=64)
+            ps = banks["z", g, h]
+            dst = zt[g][:].bitcast(F32)[:, h * G:(h + 1) * G]
+            nc.scalar.copy(out=dst.rearrange("p (t m u) -> p t m u", t=2, u=2),
+                           in_=ps[:].rearrange("p (t u m) -> p t m u", t=2, u=2))
+
+        def scale_z(g):
+            zrt[g] = work.tile([P, G * PACK], BF16, name="zrt", tag="zrt", align_bytes=64)
+            nc.vector.tensor_tensor(out=zrt[g][:].rearrange("p (n t) -> p n t", t=PACK),
+                                    in0=zt[g][:].rearrange("p (n t) -> p n t", t=PACK),
+                                    in1=rel_sb[:].unsqueeze(1).to_broadcast([P, G, PACK]), op=ALU.mult)
+
+        def quant_z(g):
+            quantize(cols(z_mx[g], 0, G), zt[g][:])
+
+        def quant_zr(g):
+            quantize(cols(zr_mx[g], 0, G), zrt[g][:])
+
+        def turn_x(g, t):
+            ps = banks["x", g, t] = bank()
+            words = x_raw[g, t // 2][:].bitcast(F32)
+            for c in range(FG):
+                for u in range(2):
+                    q = 2 * c + u
+                    lo = (t % 2) * 512 + c * 256
+                    nc.tensor.transpose(ps[:, q * P:(q + 1) * P], words[:, lo + u:lo + 256:2], ident[:])
+
+        def drain_x(g, t):
+            if t == 0:
+                xt[g] = work.tile([P, FG * G * PACK], BF16, name="xt", tag="xt", align_bytes=64)
+            ps = banks["x", g, t]
+            dst = xt[g][:].bitcast(F32).rearrange("p (c t m u) -> p c t m u", c=FG, t=PACK, u=2)[:, :, t, :, :]
+            nc.scalar.copy(out=dst, in_=ps[:].rearrange("p (c u m) -> p c m u", c=FG, u=2))
+
+        def quant_x(g):
+            quantize(cols(x_mx[g], 0, FG * G), xt[g][:])
+
+        def weave_w(og, c, on_vector):
+            wt[og, c] = work.tile([P, G * PACK], BF16, name="wt", tag="wt", align_bytes=64)
+            copy = nc.vector.tensor_copy if on_vector else nc.scalar.copy
+            copy(out=wt[og, c][:].rearrange("p (a i t) -> p a t i", i=4, t=PACK),
+                 in_=w_raw[og, c][:].rearrange("p t (a i) -> p a t i", i=4))
+            if og == 0:
+                load_w(2, c)
+
+        def quant_w(og, c):
+            quantize(cols(w_mx[og, c], 0, G), wt[og, c][:])
+
+        def scores(gj, gi, s):
+            ps = banks["p", gj, gi, s] = bank()
+            for t in range(PACK):
+                mm(ps[:, t * P:(t + 1) * P], cols(zr_mx[gj], t * P, P), cols(z_mx[gi], s * P, P), True, True)
+
+        def sigmoid(gj, gi, s):
+            if s == 0:
+                sig[gj, gi] = work.tile([P, G * PACK], F32, name="sig", tag="sig")
+            ps = banks["p", gj, gi, s]
+            nc.scalar.activation(out=sig[gj, gi][:, s * G:(s + 1) * G].rearrange("p (n t) -> p n t", t=PACK),
+                                 in_=ps[:].rearrange("p (t n) -> p n t", t=PACK), func=ACT.Sigmoid)
+
+        def scale_a(gj, gi):
+            at[gj, gi] = work.tile([P, G * PACK], BF16, name="at", tag="at", align_bytes=64)
+            nc.vector.tensor_tensor(out=at[gj, gi][:].rearrange("p (n t) -> p n t", t=PACK),
+                                    in0=sig[gj, gi][:].rearrange("p (n t) -> p n t", t=PACK),
+                                    in1=send_sb[:, gj, :].unsqueeze(1).to_broadcast([P, G, PACK]), op=ALU.mult)
+
+        def quant_a(gj, gi):
+            quantize(cols(a_mx[gj, gi], 0, G), at[gj, gi][:])
+
+        def project(og, gj, s):
+            ps = banks["v", og, gj, s] = bank()
+            for t in range(PACK):
+                for c in range(FG):
+                    mm(ps[:, t * P:(t + 1) * P], cols(x_mx[gj], c * G + t * P, P), cols(w_mx[og, c], s * P, P),
+                       c == 0, c == FG - 1)
+
+        def drain_v(og, gj, s):
+            if s == 0:
+                vt[og, gj] = work.tile([P, G * PACK], BF16, name="vt", tag="vt", align_bytes=64)
+            ps = banks["v", og, gj, s]
+            nc.scalar.copy(out=vt[og, gj][:, s * G:(s + 1) * G].rearrange("p (n t) -> p n t", t=PACK),
+                           in_=ps[:].rearrange("p (t n) -> p n t", t=PACK))
+
+        def quant_v(og, gj):
+            quantize(cols(v_mx[og, gj], 0, G), vt[og, gj][:])
+
+        def unit(k):
+            return k // (2 * NG), (k // 2) % NG, k % 2
+
+        def mix(k):
+            og, gi, h = unit(k)
+            for e in range(2):
+                t = 2 * h + e
+                ps = banks["s", k, e] = bank()
+                for gj in range(NG):
+                    mm(ps[:], cols(a_mx[gj, gi], t * P, P), cols(v_mx[og, gj], 0, G), gj == 0, gj == NG - 1)
+
+        def affine(k):
+            og, gi, h = unit(k)
+            pre[k] = work.tile([P, 2 * G], F32, name="pre", tag="pre", bufs=4)
+            for e in range(2):
+                t = 2 * h + e
+                ps = banks["s", k, e]
+                nc.vector.scalar_tensor_tensor(out=pre[k][:, e * G:(e + 1) * G], in0=ps[:], scalar=recv_sb[:, gi, t:t + 1],
+                                               in1=bias_sb[:, og * G:(og + 1) * G], op0=ALU.mult, op1=ALU.add)
+
+        def squash(k):
+            nc.scalar.activation(out=pre[k][:], in_=pre[k][:], func=ACT.Tanh)
+
+        def finish(k):
+            og, gi, h = unit(k)
+            yf[k] = work.tile([P, 2 * G], F32, name="yf", tag="yf", bufs=4)
+            nc.vector.tensor_tensor(out=yf[k][:].rearrange("p (e o) -> p e o", e=2),
+                                    in0=pre[k][:].rearrange("p (e o) -> p e o", e=2),
+                                    in1=gain_sb[:, og * G:(og + 1) * G].unsqueeze(1).to_broadcast([P, 2, G]), op=ALU.mult)
+            rows = out_0[gi * G:(gi + 1) * G, og * G:(og + 1) * G].rearrange("(m t) o -> m t o", t=PACK)
+            nc.sync.dma_start(out=rows[:, 2 * h:2 * h + 2, :], in_=yf[k][:].rearrange("p (e o) -> p e o", e=2))
+
+        def round_y(k, on_vector):
+            ys[k] = work.tile([P, 2 * G], BF16, name="ys", tag="ys", bufs=3)
+            dst = ys[k][:].rearrange("m (e u p b) -> m e u p b", e=2, u=2, b=2)
+            src = yf[k][:].rearrange("m (e p u b) -> m e u p b", e=2, u=2, b=2)
+            if on_vector:
+                nc.vector.tensor_copy(out=dst, in_=src)
+            else:
+                nc.scalar.copy(out=dst, in_=src)
+
+        def turn_y(k):
+            ps = banks["y", k] = bank()
+            words = ys[k][:].bitcast(F32)
+            for q in range(4):
+                nc.tensor.transpose(ps[:, q * P:(q + 1) * P], words[:, q * P:(q + 1) * P], ident[:])
+
+        def drain_y(k):
+            og, gi, h = unit(k)
+            if h == 0:
+                yt[og, gi] = work.tile([P, G * PACK], BF16, name="yt", tag="yt", align_bytes=64)
+            ps = banks["y", k]
+            dst = yt[og, gi][:].bitcast(F32).rearrange("p (m h q) -> p m h q", h=2, q=4)[:, :, h, :]
+            nc.scalar.copy(out=dst, in_=ps[:].rearrange("p (q m) -> p m q", q=4))
+
+        def emit_planes(og, gi):
+            codes = work.tile([P, G], U32, name="y_codes", tag="y_codes", align_bytes=64)
+            quantize((codes[:], y_scales[og][:, gi * G:(gi + 1) * G]), yt[og, gi][:])
+            dst = out_1[og].rearrange("p m t -> p (m t)").bitcast(I32)
+            nc.sync.dma_start(out=dst[:, gi * G:(gi + 1) * G], in_=codes[:].bitcast(I32))
+            if gi == NG - 1:
+                for q in range(4):
+                    nc.sync.dma_start(out=out_2[og, 4 * q:4 * q + 4, :].bitcast(I32),
+                                      in_=y_scales[og][32 * q:32 * q + 4, :].bitcast(I32))
+
+        steps = 2 * NG * OG
+
+        def four(f, *key):
+            return [(f, *key, s) for s in range(PACK)]
+
+        vector_order = [(weave_w, 0, 0, True), (scale_z, 0), (quant_z, 0), (quant_zr, 0), (scale_z, 1), (quant_w, 0, 0),
+                        (quant_zr, 1), (weave_w, 0, 1, True), (quant_z, 1),
+                        (scale_a, 0, 0), (quant_w, 0, 1), (quant_x, 0), (quant_a, 0, 0), (scale_a, 1, 0), (quant_x, 1), (quant_a, 1, 0),
+                        (weave_w, 1, 0, True), (quant_v, 0, 0), (quant_w, 1, 0), (scale_a, 0, 1), (quant_v, 0, 1), (quant_a, 0, 1)]
+        scalar_order = ([(drain_z, g, h) for g in range(NG) for h in range(2)] + four(drain_x, 0)[:2] + four(sigmoid, 0, 0)
+                        + four(drain_x, 0)[2:] + four(sigmoid, 1, 0) + four(drain_x, 1) + four(drain_v, 0, 0)
+                        + four(sigmoid, 0, 1) + four(drain_v, 0, 1) + four(sigmoid, 1, 1) + [(weave_w, 1, 1, False)])
+        tensor_order = ([(turn_z, g, h) for g in range(NG) for h in range(2)] + four(turn_x, 0)[:2] + four(scores, 0, 0)
+                        + four(turn_x, 0)[2:] + four(scores, 1, 0) + four(turn_x, 1) + four(project, 0, 0)
+                        + four(scores, 0, 1) + four(project, 0, 1) + four(scores, 1, 1) + [(mix, 0)])
+        side_v = {0: [(scale_a, 1, 1), (quant_w, 1, 1), (quant_a, 1, 1)], 2: [(quant_w, 2, 0), (quant_v, 1, 0)], 3: [(quant_v, 1, 1), (weave_w, 2, 1, True)], 4: [(quant_w, 2, 1)], 6: [(quant_v, 2, 0)], 7: [(quant_v, 2, 1)]}
+        side_s = {0: [(weave_w, 2, 0, False)]}
+        vs = [(1, gj, s) for gj in range(NG) for s in range(4)] + [(2, gj, s) for gj in range(NG) for s in range(4)]
+        side_b = {1: vs[0:4], 2: vs[4:8], 4: vs[8:10], 5: vs[10:13], 6: vs[13:16]}
+        for k in range(steps + 3):
+            cast_on_vector = k - 2 in (3, 4, 5, 10, 11)
+            late = k in ()
+            if late:
+                vector_order.extend(side_v.get(k, []))
+                vector_order.append((finish, k - 1))
+            if k < steps:
+                vector_order.append((affine, k))
+            if not late:
+                vector_order.extend(side_v.get(k, []))
+            if 0 <= k - 2 < steps and cast_on_vector:
+                vector_order.append((round_y, k - 2, True))
+            if 0 <= k - 1 < steps and not late:
+                vector_order.append((finish, k - 1))
+            if 0 <= k - 3 < steps and (k - 3) % 2 == 1:
+                vector_order.append((emit_planes, *unit(k - 3)[:2]))
+            if 0 <= k - 2 < steps and not cast_on_vector:
+                scalar_order.append((round_y, k - 2, False))
+            if k < steps:
+                scalar_order.append((squash, k))
+            scalar_order.extend([(drain_v, *b) for b in side_b.get(k, [])])
+            scalar_order.extend(side_s.get(k, []))
+            if 0 <= k - 2 < steps:
+                scalar_order.append((drain_y, k - 2))
+            tensor_order.extend([(project, *b) for b in side_b.get(k, [])])
+            if k + 1 < steps and k not in (3, 7):
+                tensor_order.append((mix, k + 1))
+            if 0 <= k - 2 < steps:
+                tensor_order.append((turn_y, k - 2))
+            if k in (3, 7):
+                tensor_order.append((mix, k + 1))
+        steps = 2 * NG * OG
+        needs = {
+            turn_z: lambda g, h: [],
+            turn_x: lambda g, t: [],
+            weave_w: lambda og, c, on_vector: [],
+            drain_z: lambda g, h: [(turn_z, g, h)],
+            drain_x: lambda g, t: [(turn_x, g, t)],
+            scale_z: lambda g: [(drain_z, g, h) for h in range(2)],
+            quant_z: lambda g: [(drain_z, g, h) for h in range(2)],
+            quant_zr: lambda g: [(scale_z, g)],
+            quant_x: lambda g: [(drain_x, g, t) for t in range(PACK)],
+            quant_w: lambda og, c: [(weave_w, og, c)],
+            scores: lambda gj, gi, s: [(quant_zr, gj), (quant_z, gi)],
+            sigmoid: lambda gj, gi, s: [(scores, gj, gi, s)],
+            scale_a: lambda gj, gi: [(sigmoid, gj, gi, s) for s in range(PACK)],
+            quant_a: lambda gj, gi: [(scale_a, gj, gi)],
+            project: lambda og, gj, s: [(quant_x, gj)] + [(quant_w, og, c) for c in range(FG)],
+            drain_v: lambda og, gj, s: [(project, og, gj, s)],
+            quant_v: lambda og, gj: [(drain_v, og, gj, s) for s in range(PACK)],
+            mix: lambda k: [(f, *key) for gj in range(NG) for f, key in ((quant_a, (gj, unit(k)[1])), (quant_v, (unit(k)[0], gj)))],
+            affine: lambda k: [(mix, k)],
+            squash: lambda k: [(affine, k)],
+            finish: lambda k: [(squash, k)],
+            round_y: lambda k, on_vector: [(finish, k)],
+            turn_y: lambda k: [(round_y, k)],
+            drain_y: lambda k: [(turn_y, k)],
+            emit_planes: lambda og, gi: [(drain_y, 2 * (NG * og + gi) + h) for h in range(2)],
+        }
+        opens = {turn_z: 1, turn_x: 1, scores: 1, project: 1, mix: 2, turn_y: 1,
+                 drain_z: -1, drain_x: -1, sigmoid: -1, drain_v: -1, affine: -2, drain_y: -1}
+        done = set()
+        queues = [vector_order, scalar_order, tensor_order]
+        place = [0, 0, 0]
+        open_banks = 0
+        while any(place[q] < len(queues[q]) for q in range(3)):
+            moved = False
+            for q in range(3):
+                if place[q] == len(queues[q]):
+                    continue
+                step = queues[q][place[q]]
+                f, key = step[0], step[1:]
+                if all(n in done for n in needs[f](*key)) and open_banks + opens.get(f, 0) <= 8:
+                    f(*key)
+                    done.add(step[:-1] if f in (weave_w, round_y) else step)
+                    open_banks = open_banks + opens.get(f, 0)
+                    place[q] = place[q] + 1
+                    moved = True
+            assert moved

@@ -21,6 +21,7 @@ G = P * PACK
 NG = NODES // G
 FG = F // G
 OG = O // G
+BANKS = {"wide": 3, "quad": 5}
 
 
 def tile_distmult_sigmoid_neighbour_mix_h3_kernel(tc, z, relation, x, w, send, recv, bias, gain, out_0, out_1, out_2):
@@ -28,10 +29,10 @@ def tile_distmult_sigmoid_neighbour_mix_h3_kernel(tc, z, relation, x, w, send, r
     with ExitStack() as ctx:
         keep = ctx.enter_context(tc.tile_pool(name="keep", bufs=1))
         work = ctx.enter_context(tc.tile_pool(name="work", bufs=2))
-        psum = ctx.enter_context(tc.psum_pool(name="psum", bufs=8))
+        psum = ctx.enter_context(tc.psum_pool(name="psum", bufs=4))
 
-        def bank():
-            return psum.tile([P, G], F32, name="bank", tag="bank")
+        def bank(tag):
+            return psum.tile([P, G], F32, name=tag, tag=tag, bufs=BANKS[tag])
 
         def mx_pair(name, width):
             codes = keep.tile([P, width], U32, name=name + "_codes", align_bytes=64)
@@ -59,6 +60,9 @@ def tile_distmult_sigmoid_neighbour_mix_h3_kernel(tc, z, relation, x, w, send, r
         nc.scalar.dma_start(out=send_sb[:], in_=send.rearrange("(g p t) -> p g t", g=NG, t=PACK))
         nc.scalar.dma_start(out=recv_sb[:], in_=recv.rearrange("(g p t) -> p g t", g=NG, t=PACK))
 
+        warm = keep.tile([P, 1], F32, name="warm")
+        nc.scalar.activation(out=warm[:], in_=ident[:, 0:1], func=ACT.Sigmoid)
+
         z_raw, x_raw, w_raw = {}, {}, {}
 
         def load_z(g, h):
@@ -77,8 +81,8 @@ def tile_distmult_sigmoid_neighbour_mix_h3_kernel(tc, z, relation, x, w, send, r
                               in_=w[c * G:(c + 1) * G, og * G:(og + 1) * G].rearrange("(p t) o -> p t o", t=PACK))
 
         load_z(0, 0)
-        load_w(0, 0)
         load_z(0, 1)
+        load_w(0, 0)
         load_z(1, 0)
         load_z(1, 1)
         load_x(0, 0)
@@ -105,7 +109,7 @@ def tile_distmult_sigmoid_neighbour_mix_h3_kernel(tc, z, relation, x, w, send, r
         zt, zrt, xt, wt, sig, at, vt, pre, yf, ys, yt = {}, {}, {}, {}, {}, {}, {}, {}, {}, {}, {}
 
         def turn_z(g, h):
-            ps = banks["z", g, h] = bank()
+            ps = banks["z", g, h] = bank("wide")
             words = z_raw[g, h][:].bitcast(F32)
             for t in range(2):
                 for u in range(2):
@@ -133,7 +137,7 @@ def tile_distmult_sigmoid_neighbour_mix_h3_kernel(tc, z, relation, x, w, send, r
             quantize(cols(zr_mx[g], 0, G), zrt[g][:])
 
         def turn_x(g, t):
-            ps = banks["x", g, t] = bank()
+            ps = banks["x", g, t] = bank("wide")
             words = x_raw[g, t // 2][:].bitcast(F32)
             for c in range(FG):
                 for u in range(2):
@@ -163,7 +167,7 @@ def tile_distmult_sigmoid_neighbour_mix_h3_kernel(tc, z, relation, x, w, send, r
             quantize(cols(w_mx[og, c], 0, G), wt[og, c][:])
 
         def scores(gj, gi, s):
-            ps = banks["p", gj, gi, s] = bank()
+            ps = banks["p", gj, gi, s] = bank("quad")
             for t in range(PACK):
                 mm(ps[:, t * P:(t + 1) * P], cols(zr_mx[gj], t * P, P), cols(z_mx[gi], s * P, P), True, True)
 
@@ -184,7 +188,7 @@ def tile_distmult_sigmoid_neighbour_mix_h3_kernel(tc, z, relation, x, w, send, r
             quantize(cols(a_mx[gj, gi], 0, G), at[gj, gi][:])
 
         def project(og, gj, s):
-            ps = banks["v", og, gj, s] = bank()
+            ps = banks["v", og, gj, s] = bank("quad")
             for t in range(PACK):
                 for c in range(FG):
                     mm(ps[:, t * P:(t + 1) * P], cols(x_mx[gj], c * G + t * P, P), cols(w_mx[og, c], s * P, P),
@@ -203,66 +207,65 @@ def tile_distmult_sigmoid_neighbour_mix_h3_kernel(tc, z, relation, x, w, send, r
         def unit(k):
             return k // (2 * NG), (k // 2) % NG, k % 2
 
-        def mix(k):
+        def mix(k, e):
             og, gi, h = unit(k)
-            for e in range(2):
-                t = 2 * h + e
-                ps = banks["s", k, e] = bank()
-                for gj in range(NG):
-                    mm(ps[:], cols(a_mx[gj, gi], t * P, P), cols(v_mx[og, gj], 0, G), gj == 0, gj == NG - 1)
+            ps = banks["s", k, e] = bank("wide")
+            for gj in range(NG):
+                mm(ps[:], cols(a_mx[gj, gi], (2 * h + e) * P, P), cols(v_mx[og, gj], 0, G), gj == 0, gj == NG - 1)
 
-        def affine(k):
+        def affine(k, e):
             og, gi, h = unit(k)
-            pre[k] = work.tile([P, 2 * G], F32, name="pre", tag="pre", bufs=4)
-            for e in range(2):
-                t = 2 * h + e
-                ps = banks["s", k, e]
-                nc.vector.scalar_tensor_tensor(out=pre[k][:, e * G:(e + 1) * G], in0=ps[:], scalar=recv_sb[:, gi, t:t + 1],
-                                               in1=bias_sb[:, og * G:(og + 1) * G], op0=ALU.mult, op1=ALU.add)
+            if e == 0:
+                pre[k] = work.tile([P, 2 * G], F32, name="pre", tag="pre", bufs=4)
+            t = 2 * h + e
+            nc.vector.scalar_tensor_tensor(out=pre[k][:, e * G:(e + 1) * G], in0=banks["s", k, e][:], scalar=recv_sb[:, gi, t:t + 1],
+                                           in1=bias_sb[:, og * G:(og + 1) * G], op0=ALU.mult, op1=ALU.add)
 
-        def squash(k):
-            nc.scalar.activation(out=pre[k][:], in_=pre[k][:], func=ACT.Tanh)
+        def squash(k, lo, hi):
+            nc.scalar.activation(out=pre[k][:, lo * G:hi * G], in_=pre[k][:, lo * G:hi * G], func=ACT.Tanh)
 
-        def finish(k):
+        def finish(k, lo, hi):
             og, gi, h = unit(k)
-            yf[k] = work.tile([P, 2 * G], F32, name="yf", tag="yf", bufs=4)
-            nc.vector.tensor_tensor(out=yf[k][:].rearrange("p (e o) -> p e o", e=2),
-                                    in0=pre[k][:].rearrange("p (e o) -> p e o", e=2),
-                                    in1=gain_sb[:, og * G:(og + 1) * G].unsqueeze(1).to_broadcast([P, 2, G]), op=ALU.mult)
+            if lo == 0:
+                yf[k] = work.tile([P, 2, G], F32, name="yf", tag="yf", bufs=4)
+            nc.vector.tensor_tensor(out=yf[k][:, lo:hi, :], in0=pre[k][:].rearrange("p (e o) -> p e o", e=2)[:, lo:hi, :],
+                                    in1=gain_sb[:, og * G:(og + 1) * G].unsqueeze(1).to_broadcast([P, hi - lo, G]), op=ALU.mult)
             rows = out_0[gi * G:(gi + 1) * G, og * G:(og + 1) * G].rearrange("(m t) o -> m t o", t=PACK)
-            nc.sync.dma_start(out=rows[:, 2 * h:2 * h + 2, :], in_=yf[k][:].rearrange("p (e o) -> p e o", e=2))
+            nc.sync.dma_start(out=rows[:, 2 * h + lo:2 * h + hi, :], in_=yf[k][:, lo:hi, :])
 
-        def round_y(k, on_vector):
-            ys[k] = work.tile([P, 2 * G], BF16, name="ys", tag="ys", bufs=3)
-            dst = ys[k][:].rearrange("m (e u p b) -> m e u p b", e=2, u=2, b=2)
-            src = yf[k][:].rearrange("m (e p u b) -> m e u p b", e=2, u=2, b=2)
-            if on_vector:
+        def round_y(k, lo, hi, engine):
+            ys[k, lo] = work.tile([P, (hi - lo) * G], BF16, name="ys", tag="ys", bufs=3)
+            dst = ys[k, lo][:].rearrange("m (u n b) -> m u n b", u=2, b=2)
+            src = yf[k][:, lo:hi, :].rearrange("m e (p u b) -> m u (e p) b", u=2, b=2)
+            if engine == "v":
                 nc.vector.tensor_copy(out=dst, in_=src)
+            elif engine == "g":
+                nc.gpsimd.tensor_scalar(out=dst, in0=src, scalar1=1.0, scalar2=0.0, op0=ALU.mult, op1=ALU.add)
             else:
                 nc.scalar.copy(out=dst, in_=src)
 
-        def turn_y(k):
-            ps = banks["y", k] = bank()
-            words = ys[k][:].bitcast(F32)
-            for q in range(4):
+        def turn_y(k, lo, hi):
+            ps = banks["y", k, lo] = bank("quad")
+            words = ys[k, lo][:].bitcast(F32)
+            for q in range(2 * (hi - lo)):
                 nc.tensor.transpose(ps[:, q * P:(q + 1) * P], words[:, q * P:(q + 1) * P], ident[:])
 
-        def drain_y(k):
+        def drain_y(k, lo, hi):
             og, gi, h = unit(k)
-            if h == 0:
+            if h == 0 and lo == 0:
                 yt[og, gi] = work.tile([P, G * PACK], BF16, name="yt", tag="yt", align_bytes=64)
-            ps = banks["y", k]
-            dst = yt[og, gi][:].bitcast(F32).rearrange("p (m h q) -> p m h q", h=2, q=4)[:, :, h, :]
-            nc.scalar.copy(out=dst, in_=ps[:].rearrange("p (q m) -> p m q", q=4))
+            dst = yt[og, gi][:].bitcast(F32).rearrange("p (m t u) -> p m t u", t=PACK, u=2)[:, :, 2 * h + lo:2 * h + hi, :]
+            nc.scalar.copy(out=dst, in_=banks["y", k, lo][:, :2 * (hi - lo) * P].rearrange("p (u e m) -> p m e u", u=2, m=P))
 
         def emit_planes(og, gi):
-            codes = work.tile([P, G], U32, name="y_codes", tag="y_codes", align_bytes=64)
+            codes = work.tile([P, G], U32, name="y_codes", tag="y_codes", bufs=3, align_bytes=64)
             quantize((codes[:], y_scales[og][:, gi * G:(gi + 1) * G]), yt[og, gi][:])
             dst = out_1[og].rearrange("p m t -> p (m t)").bitcast(I32)
             nc.sync.dma_start(out=dst[:, gi * G:(gi + 1) * G], in_=codes[:].bitcast(I32))
             if gi == NG - 1:
                 for q in range(4):
-                    nc.sync.dma_start(out=out_2[og, 4 * q:4 * q + 4, :].bitcast(I32),
+                    queue = nc.scalar if og == OG - 1 else nc.sync
+                    queue.dma_start(out=out_2[og, 4 * q:4 * q + 4, :].bitcast(I32),
                                       in_=y_scales[og][32 * q:32 * q + 4, :].bitcast(I32))
 
         steps = 2 * NG * OG
@@ -270,51 +273,70 @@ def tile_distmult_sigmoid_neighbour_mix_h3_kernel(tc, z, relation, x, w, send, r
         def four(f, *key):
             return [(f, *key, s) for s in range(PACK)]
 
+        def lead_in(z_step, x_step, p_step, v_step):
+            xs = four(x_step, 0) + four(x_step, 1)
+            ps = four(p_step, 0, 0) + four(p_step, 1, 0) + four(p_step, 0, 1) + four(p_step, 1, 1)
+            vs = four(v_step, 0, 0) + four(v_step, 0, 1)
+            order = [(z_step, g, h) for g in range(NG) for h in range(2)]
+            order = order + xs[0:1] + ps[0:4] + xs[1:3] + ps[4:6] + xs[3:4] + ps[6:8] + xs[4:6] + ps[8:10] + xs[6:8] + vs[0:4] + ps[10:12] + vs[4:8] + ps[12:16]
+            return order
+
         vector_order = [(weave_w, 0, 0, True), (scale_z, 0), (quant_z, 0), (quant_zr, 0), (scale_z, 1), (quant_w, 0, 0),
                         (quant_zr, 1), (weave_w, 0, 1, True), (quant_z, 1),
                         (scale_a, 0, 0), (quant_w, 0, 1), (quant_x, 0), (quant_a, 0, 0), (scale_a, 1, 0), (quant_x, 1), (quant_a, 1, 0),
                         (weave_w, 1, 0, True), (quant_v, 0, 0), (quant_w, 1, 0), (scale_a, 0, 1), (quant_v, 0, 1), (quant_a, 0, 1)]
-        scalar_order = ([(drain_z, g, h) for g in range(NG) for h in range(2)] + four(drain_x, 0)[:2] + four(sigmoid, 0, 0)
-                        + four(drain_x, 0)[2:] + four(sigmoid, 1, 0) + four(drain_x, 1) + four(drain_v, 0, 0)
-                        + four(sigmoid, 0, 1) + four(drain_v, 0, 1) + four(sigmoid, 1, 1) + [(weave_w, 1, 1, False)])
-        tensor_order = ([(turn_z, g, h) for g in range(NG) for h in range(2)] + four(turn_x, 0)[:2] + four(scores, 0, 0)
-                        + four(turn_x, 0)[2:] + four(scores, 1, 0) + four(turn_x, 1) + four(project, 0, 0)
-                        + four(scores, 0, 1) + four(project, 0, 1) + four(scores, 1, 1) + [(mix, 0)])
-        side_v = {0: [(scale_a, 1, 1), (quant_w, 1, 1), (quant_a, 1, 1)], 2: [(quant_w, 2, 0), (quant_v, 1, 0)], 3: [(quant_v, 1, 1), (weave_w, 2, 1, True)], 4: [(quant_w, 2, 1)], 6: [(quant_v, 2, 0)], 7: [(quant_v, 2, 1)]}
-        side_s = {0: [(weave_w, 2, 0, False)]}
+        scalar_order = lead_in(drain_z, drain_x, sigmoid, drain_v) + []
+        tensor_order = lead_in(turn_z, turn_x, scores, project) + [(mix, 0, 0), (mix, 0, 1)]
+        pool_order = []
+        side_a = {0: [(weave_w, 1, 1, True)], 1: [(weave_w, 2, 1, True)], 2: [(quant_v, 1, 0)], 3: [(quant_v, 1, 1)], 5: [(quant_v, 2, 0)], 7: [(quant_v, 2, 1)]}
+        side_v = {0: [(quant_w, 1, 1), (scale_a, 1, 1), (quant_w, 2, 0)], 1: [(quant_w, 2, 1)]}
+        side_s = {}
         vs = [(1, gj, s) for gj in range(NG) for s in range(4)] + [(2, gj, s) for gj in range(NG) for s in range(4)]
-        side_b = {1: vs[0:4], 2: vs[4:8], 4: vs[8:10], 5: vs[10:13], 6: vs[13:16]}
-        for k in range(steps + 3):
-            cast_on_vector = k - 2 in (3, 4, 5, 10, 11)
-            late = k in ()
-            if late:
-                vector_order.extend(side_v.get(k, []))
-                vector_order.append((finish, k - 1))
+        side_b = {0: vs[0:4], 1: vs[4:8], 2: vs[8:10], 3: vs[10:12], 4: vs[12:14], 5: vs[14:16]}
+        dv = [(drain_v, *b) for b in vs]
+        side_p = {0: [(weave_w, 2, 0, False)], 1: dv[4:6], 3: dv[8:10], 4: dv[10:12], 5: dv[12:14], 6: dv[14:16]}
+        side_q = {0: dv[0:4], 1: dv[6:8]}
+        side_w = {0: [(quant_a, 1, 1)]}
+        for k in range(steps - 1):
+            eng = "v" if k - 1 in (4, 8) else "s"
             if k < steps:
-                vector_order.append((affine, k))
-            if not late:
-                vector_order.extend(side_v.get(k, []))
-            if 0 <= k - 2 < steps and cast_on_vector:
-                vector_order.append((round_y, k - 2, True))
-            if 0 <= k - 1 < steps and not late:
-                vector_order.append((finish, k - 1))
+                vector_order.append((affine, k, 0))
+            vector_order.extend(side_a.get(k, []))
+            if 0 <= k - 2 < steps and k - 2 in (4, 8):
+                vector_order.append((round_y, k - 2, 0, 2, "v"))
+            if k < steps:
+                vector_order.append((affine, k, 1))
+            vector_order.extend(side_v.get(k, []))
+            if 0 <= k - 1 < steps:
+                vector_order.append((finish, k - 1, 0, 2))
+            vector_order.extend(side_w.get(k, []))
             if 0 <= k - 3 < steps and (k - 3) % 2 == 1:
                 vector_order.append((emit_planes, *unit(k - 3)[:2]))
-            if 0 <= k - 2 < steps and not cast_on_vector:
-                scalar_order.append((round_y, k - 2, False))
+            scalar_order.extend(side_p.get(k, []))
             if k < steps:
-                scalar_order.append((squash, k))
-            scalar_order.extend([(drain_v, *b) for b in side_b.get(k, [])])
+                scalar_order.append((squash, k, 0, 2))
+            scalar_order.extend(side_q.get(k, []))
+            if 0 <= k - 1 < steps and eng == "s":
+                scalar_order.append((round_y, k - 1, 0, 2, eng))
             scalar_order.extend(side_s.get(k, []))
             if 0 <= k - 2 < steps:
-                scalar_order.append((drain_y, k - 2))
-            tensor_order.extend([(project, *b) for b in side_b.get(k, [])])
-            if k + 1 < steps and k not in (3, 7):
-                tensor_order.append((mix, k + 1))
+                scalar_order.append((drain_y, k - 2, 0, 2))
+            sb = [(project, *b) for b in side_b.get(k, [])]
+            if k + 1 < steps:
+                tensor_order.append((mix, k + 1, 0))
+            tensor_order.extend(sb[:2])
             if 0 <= k - 2 < steps:
-                tensor_order.append((turn_y, k - 2))
-            if k in (3, 7):
-                tensor_order.append((mix, k + 1))
+                tensor_order.append((turn_y, k - 2, 0, 2))
+            if k + 1 < steps:
+                tensor_order.append((mix, k + 1, 1))
+            tensor_order.extend(sb[2:])
+        k = steps - 1
+        vector_order.extend([(affine, k, 0), (affine, k, 1), (finish, k - 1, 0, 2), (finish, k, 0, 1),
+                             (round_y, k - 1, 0, 2, "v"), (finish, k, 1, 2), (round_y, k, 0, 1, "v"), (emit_planes, 2, 0),
+                             (round_y, k, 1, 2, "v"), (emit_planes, 2, 1)])
+        scalar_order.extend([(squash, k, 0, 1), (squash, k, 1, 2), (drain_y, k - 2, 0, 2), (drain_y, k - 1, 0, 2),
+                             (drain_y, k, 0, 1), (drain_y, k, 1, 2)])
+        tensor_order.extend([(turn_y, k - 2, 0, 2), (turn_y, k - 1, 0, 2), (turn_y, k, 0, 1), (turn_y, k, 1, 2)])
         steps = 2 * NG * OG
         needs = {
             turn_z: lambda g, h: [],
@@ -334,32 +356,39 @@ def tile_distmult_sigmoid_neighbour_mix_h3_kernel(tc, z, relation, x, w, send, r
             project: lambda og, gj, s: [(quant_x, gj)] + [(quant_w, og, c) for c in range(FG)],
             drain_v: lambda og, gj, s: [(project, og, gj, s)],
             quant_v: lambda og, gj: [(drain_v, og, gj, s) for s in range(PACK)],
-            mix: lambda k: [(f, *key) for gj in range(NG) for f, key in ((quant_a, (gj, unit(k)[1])), (quant_v, (unit(k)[0], gj)))],
-            affine: lambda k: [(mix, k)],
-            squash: lambda k: [(affine, k)],
-            finish: lambda k: [(squash, k)],
-            round_y: lambda k, on_vector: [(finish, k)],
-            turn_y: lambda k: [(round_y, k)],
-            drain_y: lambda k: [(turn_y, k)],
-            emit_planes: lambda og, gi: [(drain_y, 2 * (NG * og + gi) + h) for h in range(2)],
+            mix: lambda k, e: [(f, *key) for gj in range(NG) for f, key in ((quant_a, (gj, unit(k)[1])), (quant_v, (unit(k)[0], gj)))],
+            affine: lambda k, e: [(mix, k, e)],
+            squash: lambda k, lo, hi: [(affine, k, e) for e in range(lo, hi)],
+            finish: lambda k, lo, hi: [(squash, k, e) for e in range(lo, hi)],
+            round_y: lambda k, lo, hi, engine: [(finish, k, e) for e in range(lo, hi)],
+            turn_y: lambda k, lo, hi: [(round_y, k, e) for e in range(lo, hi)],
+            drain_y: lambda k, lo, hi: [(turn_y, k, e) for e in range(lo, hi)],
+            emit_planes: lambda og, gi: [(drain_y, 2 * (NG * og + gi) + h, e) for h in range(2) for e in range(2)],
         }
-        opens = {turn_z: 1, turn_x: 1, scores: 1, project: 1, mix: 2, turn_y: 1,
-                 drain_z: -1, drain_x: -1, sigmoid: -1, drain_v: -1, affine: -2, drain_y: -1}
+        opens = {turn_z: "wide", turn_x: "wide", mix: "wide", scores: "quad", project: "quad", turn_y: "quad"}
+        closes = {drain_z: "wide", drain_x: "wide", affine: "wide", sigmoid: "quad", drain_v: "quad", drain_y: "quad"}
+        free = {"wide": BANKS["wide"], "quad": BANKS["quad"], None: 1}
         done = set()
-        queues = [vector_order, scalar_order, tensor_order]
-        place = [0, 0, 0]
-        open_banks = 0
-        while any(place[q] < len(queues[q]) for q in range(3)):
+        queues = [vector_order, scalar_order, tensor_order, pool_order]
+        place = [0, 0, 0, 0]
+        while any(place[q] < len(queues[q]) for q in range(4)):
             moved = False
-            for q in range(3):
+            for q in range(4):
                 if place[q] == len(queues[q]):
                     continue
                 step = queues[q][place[q]]
                 f, key = step[0], step[1:]
-                if all(n in done for n in needs[f](*key)) and open_banks + opens.get(f, 0) <= 8:
+                if all(n in done for n in needs[f](*key)) and free[opens.get(f)] > 0:
                     f(*key)
-                    done.add(step[:-1] if f in (weave_w, round_y) else step)
-                    open_banks = open_banks + opens.get(f, 0)
+                    if f in (squash, finish, round_y, turn_y, drain_y):
+                        for e in range(key[1], key[2]):
+                            done.add((f, key[0], e))
+                    else:
+                        done.add(step[:-1] if f == weave_w else step)
+                    if f in opens:
+                        free[opens[f]] = free[opens[f]] - 1
+                    if f in closes:
+                        free[closes[f]] = free[closes[f]] + 1
                     place[q] = place[q] + 1
                     moved = True
             assert moved

@@ -18,38 +18,48 @@ ALU = mybir.AluOpType
 P = 128
 PACK = 4
 G = P * PACK
+H = G // 2
 NG = NODES // G
 FG = F // G
 OG = O // G
+PAIRS = 2 * NG * OG
+
 BANKS = {"wide": 3, "quad": 5}
+ROUND_ON_VECTOR = range(1, 4)
 
 
-def tile_distmult_sigmoid_neighbour_mix_h3_kernel(tc, z, relation, x, w, send, recv, bias, gain, out_0, out_1, out_2):
+def tile_distmult_sigmoid_neighbour_mix_h3_kernel(
+    tc, z, relation, x, w, send, recv, bias, gain, out_0, out_1, out_2
+):
     nc = tc.nc
     with ExitStack() as ctx:
         keep = ctx.enter_context(tc.tile_pool(name="keep", bufs=1))
         work = ctx.enter_context(tc.tile_pool(name="work", bufs=2))
-        psum = ctx.enter_context(tc.psum_pool(name="psum", bufs=4))
+        psum = ctx.enter_context(tc.psum_pool(name="psum", bufs=1))
+        ctx.enter_context(tc.manual_schedule())
+        on_vector, on_scalar = nc.vector.tensor_copy, nc.scalar.copy
 
         def bank(tag):
             return psum.tile([P, G], F32, name=tag, tag=tag, bufs=BANKS[tag])
 
-        def mx_pair(name, width):
+        def woven(tag, bufs=2, groups=1):
+            return work.tile([P, groups * G * PACK], BF16, name=tag, tag=tag, bufs=bufs, align_bytes=64)
+
+        def mx_operand(name, width):
             codes = keep.tile([P, width], U32, name=name + "_codes", align_bytes=64)
             scales = keep.tile([P, width], U8, name=name + "_scales", align_bytes=64)
             return codes, scales
 
-        def quantize(pair, src):
-            nc.vector.quantize_mx(out=pair[0].bitcast(FP8X4), scales=pair[1], in_=src)
+        def cols(operand, first, n):
+            return operand[0][:, first:first + n], operand[1][:, first:first + n]
 
-        def mm(out, lhs, rhs, start, stop):
-            nc.tensor.matmul_mx(out=out, lhsT=lhs[0].bitcast(FP8X4), lhsT_scale=lhs[1],
-                                rhs=rhs[0].bitcast(FP8X4), rhs_scale=rhs[1], start=start, stop=stop)
+        def quantize(operand, src):
+            nc.vector.quantize_mx(out=operand[0].bitcast(FP8X4), scales=operand[1], in_=src)
 
-        def cols(pair, lo, n):
-            return pair[0][:, lo:lo + n], pair[1][:, lo:lo + n]
+        def matmul(out, stationary, moving, start, stop):
+            nc.tensor.matmul_mx(out=out, lhsT=stationary[0].bitcast(FP8X4), lhsT_scale=stationary[1],
+                                rhs=moving[0].bitcast(FP8X4), rhs_scale=moving[1], start=start, stop=stop)
 
-        ctx.enter_context(tc.manual_schedule())
         ident = keep.tile([P, P], F32, name="ident")
         make_identity(nc, ident[:])
 
@@ -75,38 +85,39 @@ def tile_distmult_sigmoid_neighbour_mix_h3_kernel(tc, z, relation, x, w, send, r
             rows = x[g * G:(g + 1) * G, :].rearrange("(m t) f -> m (t f)", t=PACK)
             nc.sync.dma_start(out=x_raw[g, h][:], in_=rows[:, 2 * h * F:2 * (h + 1) * F])
 
-        def load_w(og, c):
-            w_raw[og, c] = work.tile([P, PACK, G], BF16, name="w_raw", tag="w_raw", bufs=4)
-            nc.sync.dma_start(out=w_raw[og, c][:],
-                              in_=w[c * G:(c + 1) * G, og * G:(og + 1) * G].rearrange("(p t) o -> p t o", t=PACK))
+        def load_w(og, c, lo, hi):
+            w_raw[og, c, lo] = work.tile([P, PACK, (hi - lo) * H], BF16, name="w_raw", tag="w_raw", bufs=5)
+            block = w[c * G:(c + 1) * G, og * G + lo * H:og * G + hi * H]
+            nc.sync.dma_start(out=w_raw[og, c, lo][:], in_=block.rearrange("(p t) o -> p t o", t=PACK))
 
-        load_z(0, 0)
-        load_z(0, 1)
-        load_w(0, 0)
-        load_z(1, 0)
-        load_z(1, 1)
-        load_x(0, 0)
-        load_x(0, 1)
-        load_w(0, 1)
-        load_x(1, 0)
-        load_x(1, 1)
-        load_w(1, 0)
-        load_w(1, 1)
+        for h in range(2):
+            load_w(0, 0, h, h + 1)
+            load_z(0, h)
+        for h in range(2):
+            load_z(1, h)
+        for h in range(2):
+            load_x(0, h)
+        load_w(0, 1, 0, 2)
+        for h in range(2):
+            load_x(1, h)
+        for c in range(FG):
+            load_w(1, c, 0, 2)
         bias_sb = keep.tile([P, O], BF16, name="bias_sb")
         gain_sb = keep.tile([P, O], BF16, name="gain_sb")
         nc.sync.dma_start(out=bias_sb[:], in_=bias.partition_broadcast(P))
         nc.sync.dma_start(out=gain_sb[:], in_=gain.partition_broadcast(P))
 
-        z_mx = [mx_pair("z%d" % g, G) for g in range(NG)]
-        zr_mx = [mx_pair("zr%d" % g, G) for g in range(NG)]
-        x_mx = [mx_pair("x%d" % g, FG * G) for g in range(NG)]
-        w_mx = {(og, c): mx_pair("w%d%d" % (og, c), G) for og in range(OG) for c in range(FG)}
-        a_mx = {(gj, gi): mx_pair("a%d%d" % (gj, gi), G) for gj in range(NG) for gi in range(NG)}
-        v_mx = {(og, gj): mx_pair("v%d%d" % (og, gj), G) for og in range(OG) for gj in range(NG)}
+        z_mx = [mx_operand("z%d" % g, G) for g in range(NG)]
+        zr_mx = [mx_operand("zr%d" % g, G) for g in range(NG)]
+        x_mx = [mx_operand("x%d" % g, FG * G) for g in range(NG)]
+        w_mx = {(og, c): mx_operand("w%d%d" % (og, c), G) for og in range(OG) for c in range(FG)}
+        a_mx = {(gj, gi): mx_operand("a%d%d" % (gj, gi), G) for gj in range(NG) for gi in range(NG)}
+        v_mx = {(og, gj): mx_operand("v%d%d" % (og, gj), G) for og in range(OG) for gj in range(NG)}
         y_scales = [keep.tile([P, NODES], U8, name="y_scales%d" % og, align_bytes=64) for og in range(OG)]
 
         banks = {}
         zt, zrt, xt, wt, sig, at, vt, pre, yf, ys, yt = {}, {}, {}, {}, {}, {}, {}, {}, {}, {}, {}
+
 
         def turn_z(g, h):
             ps = banks["z", g, h] = bank("wide")
@@ -114,27 +125,28 @@ def tile_distmult_sigmoid_neighbour_mix_h3_kernel(tc, z, relation, x, w, send, r
             for t in range(2):
                 for u in range(2):
                     q = 2 * t + u
-                    nc.tensor.transpose(ps[:, q * P:(q + 1) * P], words[:, t * 256 + u:(t + 1) * 256:2], ident[:])
+                    nc.tensor.transpose(ps[:, q * P:(q + 1) * P], words[:, t * H + u:(t + 1) * H:2], ident[:])
 
         def drain_z(g, h):
             if h == 0:
-                zt[g] = work.tile([P, G * PACK], BF16, name="zt", tag="zt", align_bytes=64)
-            ps = banks["z", g, h]
+                zt[g] = woven("zt")
             dst = zt[g][:].bitcast(F32)[:, h * G:(h + 1) * G]
             nc.scalar.copy(out=dst.rearrange("p (t m u) -> p t m u", t=2, u=2),
-                           in_=ps[:].rearrange("p (t u m) -> p t m u", t=2, u=2))
+                           in_=banks["z", g, h][:].rearrange("p (t u m) -> p t m u", t=2, u=2))
 
-        def scale_z(g):
-            zrt[g] = work.tile([P, G * PACK], BF16, name="zrt", tag="zrt", align_bytes=64)
-            nc.vector.tensor_tensor(out=zrt[g][:].rearrange("p (n t) -> p n t", t=PACK),
-                                    in0=zt[g][:].rearrange("p (n t) -> p n t", t=PACK),
-                                    in1=rel_sb[:].unsqueeze(1).to_broadcast([P, G, PACK]), op=ALU.mult)
+        def scale_z(g, lo, hi):
+            if lo == 0:
+                zrt[g] = woven("zrt", bufs=1)
+            part = slice(lo * H * PACK, hi * H * PACK)
+            nc.vector.tensor_tensor(out=zrt[g][:, part].rearrange("p (n t) -> p n t", t=PACK),
+                                    in0=zt[g][:, part].rearrange("p (n t) -> p n t", t=PACK),
+                                    in1=rel_sb[:].unsqueeze(1).to_broadcast([P, (hi - lo) * H, PACK]), op=ALU.mult)
 
-        def quant_z(g):
-            quantize(cols(z_mx[g], 0, G), zt[g][:])
+        def quant_z(g, lo, hi):
+            quantize(cols(z_mx[g], lo * H, (hi - lo) * H), zt[g][:, lo * H * PACK:hi * H * PACK])
 
-        def quant_zr(g):
-            quantize(cols(zr_mx[g], 0, G), zrt[g][:])
+        def quant_zr(g, lo, hi):
+            quantize(cols(zr_mx[g], lo * H, (hi - lo) * H), zrt[g][:, lo * H * PACK:hi * H * PACK])
 
         def turn_x(g, t):
             ps = banks["x", g, t] = bank("wide")
@@ -142,44 +154,42 @@ def tile_distmult_sigmoid_neighbour_mix_h3_kernel(tc, z, relation, x, w, send, r
             for c in range(FG):
                 for u in range(2):
                     q = 2 * c + u
-                    lo = (t % 2) * 512 + c * 256
-                    nc.tensor.transpose(ps[:, q * P:(q + 1) * P], words[:, lo + u:lo + 256:2], ident[:])
+                    first = ((t % 2) * FG + c) * H
+                    nc.tensor.transpose(ps[:, q * P:(q + 1) * P], words[:, first + u:first + H:2], ident[:])
 
         def drain_x(g, t):
             if t == 0:
-                xt[g] = work.tile([P, FG * G * PACK], BF16, name="xt", tag="xt", align_bytes=64)
-            ps = banks["x", g, t]
+                xt[g] = woven("xt", groups=FG)
             dst = xt[g][:].bitcast(F32).rearrange("p (c t m u) -> p c t m u", c=FG, t=PACK, u=2)[:, :, t, :, :]
-            nc.scalar.copy(out=dst, in_=ps[:].rearrange("p (c u m) -> p c m u", c=FG, u=2))
+            nc.scalar.copy(out=dst, in_=banks["x", g, t][:].rearrange("p (c u m) -> p c m u", c=FG, u=2))
 
         def quant_x(g):
             quantize(cols(x_mx[g], 0, FG * G), xt[g][:])
 
-        def weave_w(og, c, on_vector):
-            wt[og, c] = work.tile([P, G * PACK], BF16, name="wt", tag="wt", align_bytes=64)
-            copy = nc.vector.tensor_copy if on_vector else nc.scalar.copy
-            copy(out=wt[og, c][:].rearrange("p (a i t) -> p a t i", i=4, t=PACK),
-                 in_=w_raw[og, c][:].rearrange("p t (a i) -> p a t i", i=4))
-            if og == 0:
-                load_w(2, c)
+        def weave_w(og, c, copy, lo, hi):
+            if lo == 0:
+                wt[og, c] = woven("wt", bufs=3)
+            copy(out=wt[og, c][:, lo * H * PACK:hi * H * PACK].rearrange("p (a i t) -> p a t i", i=4, t=PACK),
+                 in_=w_raw[og, c, lo][:].rearrange("p t (a i) -> p a t i", i=4))
+            if og == 0 and hi == 2:
+                load_w(OG - 1, c, 0, 2)
 
-        def quant_w(og, c):
-            quantize(cols(w_mx[og, c], 0, G), wt[og, c][:])
+        def quant_w(og, c, lo, hi):
+            quantize(cols(w_mx[og, c], lo * H, (hi - lo) * H), wt[og, c][:, lo * H * PACK:hi * H * PACK])
 
         def scores(gj, gi, s):
             ps = banks["p", gj, gi, s] = bank("quad")
             for t in range(PACK):
-                mm(ps[:, t * P:(t + 1) * P], cols(zr_mx[gj], t * P, P), cols(z_mx[gi], s * P, P), True, True)
+                matmul(ps[:, t * P:(t + 1) * P], cols(zr_mx[gj], t * P, P), cols(z_mx[gi], s * P, P), True, True)
 
         def sigmoid(gj, gi, s):
             if s == 0:
                 sig[gj, gi] = work.tile([P, G * PACK], F32, name="sig", tag="sig")
-            ps = banks["p", gj, gi, s]
             nc.scalar.activation(out=sig[gj, gi][:, s * G:(s + 1) * G].rearrange("p (n t) -> p n t", t=PACK),
-                                 in_=ps[:].rearrange("p (t n) -> p n t", t=PACK), func=ACT.Sigmoid)
+                                 in_=banks["p", gj, gi, s][:].rearrange("p (t n) -> p n t", t=PACK), func=ACT.Sigmoid)
 
         def scale_a(gj, gi):
-            at[gj, gi] = work.tile([P, G * PACK], BF16, name="at", tag="at", align_bytes=64)
+            at[gj, gi] = woven("at")
             nc.vector.tensor_tensor(out=at[gj, gi][:].rearrange("p (n t) -> p n t", t=PACK),
                                     in0=sig[gj, gi][:].rearrange("p (n t) -> p n t", t=PACK),
                                     in1=send_sb[:, gj, :].unsqueeze(1).to_broadcast([P, G, PACK]), op=ALU.mult)
@@ -191,58 +201,54 @@ def tile_distmult_sigmoid_neighbour_mix_h3_kernel(tc, z, relation, x, w, send, r
             ps = banks["v", og, gj, s] = bank("quad")
             for t in range(PACK):
                 for c in range(FG):
-                    mm(ps[:, t * P:(t + 1) * P], cols(x_mx[gj], c * G + t * P, P), cols(w_mx[og, c], s * P, P),
-                       c == 0, c == FG - 1)
+                    matmul(ps[:, t * P:(t + 1) * P], cols(x_mx[gj], c * G + t * P, P), cols(w_mx[og, c], s * P, P),
+                           c == 0, c == FG - 1)
 
         def drain_v(og, gj, s):
             if s == 0:
-                vt[og, gj] = work.tile([P, G * PACK], BF16, name="vt", tag="vt", align_bytes=64)
-            ps = banks["v", og, gj, s]
+                vt[og, gj] = woven("vt")
             nc.scalar.copy(out=vt[og, gj][:, s * G:(s + 1) * G].rearrange("p (n t) -> p n t", t=PACK),
-                           in_=ps[:].rearrange("p (t n) -> p n t", t=PACK))
+                           in_=banks["v", og, gj, s][:].rearrange("p (t n) -> p n t", t=PACK))
 
         def quant_v(og, gj):
             quantize(cols(v_mx[og, gj], 0, G), vt[og, gj][:])
 
-        def unit(k):
+        def place_of(k):
             return k // (2 * NG), (k // 2) % NG, k % 2
 
         def mix(k, e):
-            og, gi, h = unit(k)
+            og, gi, h = place_of(k)
             ps = banks["s", k, e] = bank("wide")
             for gj in range(NG):
-                mm(ps[:], cols(a_mx[gj, gi], (2 * h + e) * P, P), cols(v_mx[og, gj], 0, G), gj == 0, gj == NG - 1)
+                matmul(ps[:], cols(a_mx[gj, gi], (2 * h + e) * P, P), cols(v_mx[og, gj], 0, G), gj == 0, gj == NG - 1)
 
         def affine(k, e):
-            og, gi, h = unit(k)
+            og, gi, h = place_of(k)
             if e == 0:
                 pre[k] = work.tile([P, 2 * G], F32, name="pre", tag="pre", bufs=4)
             t = 2 * h + e
-            nc.vector.scalar_tensor_tensor(out=pre[k][:, e * G:(e + 1) * G], in0=banks["s", k, e][:], scalar=recv_sb[:, gi, t:t + 1],
-                                           in1=bias_sb[:, og * G:(og + 1) * G], op0=ALU.mult, op1=ALU.add)
+            nc.vector.scalar_tensor_tensor(out=pre[k][:, e * G:(e + 1) * G], in0=banks["s", k, e][:],
+                                           scalar=recv_sb[:, gi, t:t + 1], in1=bias_sb[:, og * G:(og + 1) * G],
+                                           op0=ALU.mult, op1=ALU.add)
 
         def squash(k, lo, hi):
             nc.scalar.activation(out=pre[k][:, lo * G:hi * G], in_=pre[k][:, lo * G:hi * G], func=ACT.Tanh)
 
         def finish(k, lo, hi):
-            og, gi, h = unit(k)
+            og, gi, h = place_of(k)
             if lo == 0:
                 yf[k] = work.tile([P, 2, G], F32, name="yf", tag="yf", bufs=4)
-            nc.vector.tensor_tensor(out=yf[k][:, lo:hi, :], in0=pre[k][:].rearrange("p (e o) -> p e o", e=2)[:, lo:hi, :],
-                                    in1=gain_sb[:, og * G:(og + 1) * G].unsqueeze(1).to_broadcast([P, hi - lo, G]), op=ALU.mult)
+            nc.vector.tensor_tensor(out=yf[k][:, lo:hi, :],
+                                    in0=pre[k][:].rearrange("p (e o) -> p e o", e=2)[:, lo:hi, :],
+                                    in1=gain_sb[:, og * G:(og + 1) * G].unsqueeze(1).to_broadcast([P, hi - lo, G]),
+                                    op=ALU.mult)
             rows = out_0[gi * G:(gi + 1) * G, og * G:(og + 1) * G].rearrange("(m t) o -> m t o", t=PACK)
             nc.sync.dma_start(out=rows[:, 2 * h + lo:2 * h + hi, :], in_=yf[k][:, lo:hi, :])
 
-        def round_y(k, lo, hi, engine):
+        def round_y(k, copy, lo, hi):
             ys[k, lo] = work.tile([P, (hi - lo) * G], BF16, name="ys", tag="ys", bufs=3)
-            dst = ys[k, lo][:].rearrange("m (u n b) -> m u n b", u=2, b=2)
-            src = yf[k][:, lo:hi, :].rearrange("m e (p u b) -> m u (e p) b", u=2, b=2)
-            if engine == "v":
-                nc.vector.tensor_copy(out=dst, in_=src)
-            elif engine == "g":
-                nc.gpsimd.tensor_scalar(out=dst, in0=src, scalar1=1.0, scalar2=0.0, op0=ALU.mult, op1=ALU.add)
-            else:
-                nc.scalar.copy(out=dst, in_=src)
+            copy(out=ys[k, lo][:].rearrange("m (u n b) -> m u n b", u=2, b=2),
+                 in_=yf[k][:, lo:hi, :].rearrange("m e (p u b) -> m u (e p) b", u=2, b=2))
 
         def turn_y(k, lo, hi):
             ps = banks["y", k, lo] = bank("quad")
@@ -251,144 +257,154 @@ def tile_distmult_sigmoid_neighbour_mix_h3_kernel(tc, z, relation, x, w, send, r
                 nc.tensor.transpose(ps[:, q * P:(q + 1) * P], words[:, q * P:(q + 1) * P], ident[:])
 
         def drain_y(k, lo, hi):
-            og, gi, h = unit(k)
-            if h == 0 and lo == 0:
-                yt[og, gi] = work.tile([P, G * PACK], BF16, name="yt", tag="yt", align_bytes=64)
-            dst = yt[og, gi][:].bitcast(F32).rearrange("p (m t u) -> p m t u", t=PACK, u=2)[:, :, 2 * h + lo:2 * h + hi, :]
-            nc.scalar.copy(out=dst, in_=banks["y", k, lo][:, :2 * (hi - lo) * P].rearrange("p (u e m) -> p m e u", u=2, m=P))
+            og, gi, h = place_of(k)
+            if (og, gi) not in yt:
+                yt[og, gi] = woven("yt")
+            dst = yt[og, gi][:].bitcast(F32).rearrange("p (m t u) -> p m t u", t=PACK, u=2)
+            src = banks["y", k, lo][:, :2 * (hi - lo) * P].rearrange("p (u e m) -> p m e u", u=2, m=P)
+            nc.scalar.copy(out=dst[:, :, 2 * h + lo:2 * h + hi, :], in_=src)
 
         def emit_planes(og, gi):
             codes = work.tile([P, G], U32, name="y_codes", tag="y_codes", bufs=3, align_bytes=64)
             quantize((codes[:], y_scales[og][:, gi * G:(gi + 1) * G]), yt[og, gi][:])
-            dst = out_1[og].rearrange("p m t -> p (m t)").bitcast(I32)
-            nc.sync.dma_start(out=dst[:, gi * G:(gi + 1) * G], in_=codes[:].bitcast(I32))
+            words = out_1[og].rearrange("p m t -> p (m t)").bitcast(I32)
+            nc.sync.dma_start(out=words[:, gi * G:(gi + 1) * G], in_=codes[:].bitcast(I32))
             if gi == NG - 1:
+                queue = nc.scalar if og == OG - 1 else nc.sync
                 for q in range(4):
-                    queue = nc.scalar if og == OG - 1 else nc.sync
                     queue.dma_start(out=out_2[og, 4 * q:4 * q + 4, :].bitcast(I32),
-                                      in_=y_scales[og][32 * q:32 * q + 4, :].bitcast(I32))
+                                    in_=y_scales[og][32 * q:32 * q + 4, :].bitcast(I32))
 
-        steps = 2 * NG * OG
 
-        def four(f, *key):
-            return [(f, *key, s) for s in range(PACK)]
+        def quarters(step, *key):
+            return [(step, *key, s) for s in range(PACK)]
 
         def lead_in(z_step, x_step, p_step, v_step):
-            xs = four(x_step, 0) + four(x_step, 1)
-            ps = four(p_step, 0, 0) + four(p_step, 1, 0) + four(p_step, 0, 1) + four(p_step, 1, 1)
-            vs = four(v_step, 0, 0) + four(v_step, 0, 1)
-            order = [(z_step, g, h) for g in range(NG) for h in range(2)]
-            order = order + xs[0:1] + ps[0:4] + xs[1:3] + ps[4:6] + xs[3:4] + ps[6:8] + xs[4:6] + ps[8:10] + xs[6:8] + vs[0:4] + ps[10:12] + vs[4:8] + ps[12:16]
-            return order
+            xs = quarters(x_step, 0) + quarters(x_step, 1)
+            ps = [s for gi in range(NG) for gj in range(NG) for s in quarters(p_step, gj, gi)]
+            order = [(z_step, g, h) for g in range(NG) for h in range(2)] + ps[:4]
+            for n in range(4):
+                order = order + xs[2 * n:2 * n + 2] + ps[4 + 2 * n:6 + 2 * n]
+            return order + quarters(v_step, 0, 0) + quarters(v_step, 0, 1) + ps[12:]
 
-        vector_order = [(weave_w, 0, 0, True), (scale_z, 0), (quant_z, 0), (quant_zr, 0), (scale_z, 1), (quant_w, 0, 0),
-                        (quant_zr, 1), (weave_w, 0, 1, True), (quant_z, 1),
-                        (scale_a, 0, 0), (quant_w, 0, 1), (quant_x, 0), (quant_a, 0, 0), (scale_a, 1, 0), (quant_x, 1), (quant_a, 1, 0),
-                        (weave_w, 1, 0, True), (quant_v, 0, 0), (quant_w, 1, 0), (scale_a, 0, 1), (quant_v, 0, 1), (quant_a, 0, 1)]
-        scalar_order = lead_in(drain_z, drain_x, sigmoid, drain_v) + []
-        tensor_order = lead_in(turn_z, turn_x, scores, project) + [(mix, 0, 0), (mix, 0, 1)]
-        pool_order = []
-        side_a = {0: [(weave_w, 1, 1, True)], 1: [(weave_w, 2, 1, True)], 2: [(quant_v, 1, 0)], 3: [(quant_v, 1, 1)], 5: [(quant_v, 2, 0)], 7: [(quant_v, 2, 1)]}
-        side_v = {0: [(quant_w, 1, 1), (scale_a, 1, 1), (quant_w, 2, 0)], 1: [(quant_w, 2, 1)]}
-        side_s = {}
-        vs = [(1, gj, s) for gj in range(NG) for s in range(4)] + [(2, gj, s) for gj in range(NG) for s in range(4)]
-        side_b = {0: vs[0:4], 1: vs[4:8], 2: vs[8:10], 3: vs[10:12], 4: vs[12:14], 5: vs[14:16]}
-        dv = [(drain_v, *b) for b in vs]
-        side_p = {0: [(weave_w, 2, 0, False)], 1: dv[4:6], 3: dv[8:10], 4: dv[10:12], 5: dv[12:14], 6: dv[14:16]}
-        side_q = {0: dv[0:4], 1: dv[6:8]}
-        side_w = {0: [(quant_a, 1, 1)]}
-        for k in range(steps - 1):
-            eng = "v" if k - 1 in (4, 8) else "s"
-            if k < steps:
-                vector_order.append((affine, k, 0))
-            vector_order.extend(side_a.get(k, []))
-            if 0 <= k - 2 < steps and k - 2 in (4, 8):
-                vector_order.append((round_y, k - 2, 0, 2, "v"))
-            if k < steps:
-                vector_order.append((affine, k, 1))
-            vector_order.extend(side_v.get(k, []))
-            if 0 <= k - 1 < steps:
+        vector_order = [
+            (weave_w, 0, 0, on_vector, 0, 1), (quant_w, 0, 0, 0, 1), (weave_w, 0, 0, on_vector, 1, 2),
+            (scale_z, 0, 0, 1), (quant_w, 0, 0, 1, 2), (quant_z, 0, 0, 1), (quant_zr, 0, 0, 1),
+            (scale_z, 0, 1, 2), (quant_z, 0, 1, 2), (quant_zr, 0, 1, 2),
+            (scale_z, 1, 0, 2), (quant_z, 1, 0, 2), (quant_zr, 1, 0, 2),
+            (weave_w, 0, 1, on_vector, 0, 2), (scale_a, 0, 0), (quant_w, 0, 1, 0, 2), (quant_x, 0), (quant_a, 0, 0),
+            (scale_a, 1, 0), (quant_x, 1), (quant_a, 1, 0),
+            (weave_w, 1, 0, on_vector, 0, 2), (quant_v, 0, 0), (quant_w, 1, 0, 0, 2),
+            (scale_a, 0, 1), (quant_v, 0, 1), (quant_a, 0, 1), (weave_w, 1, 1, on_vector, 0, 2),
+        ]
+        scalar_order = lead_in(drain_z, drain_x, sigmoid, drain_v) + [(weave_w, OG - 1, c, on_scalar, 0, 2) for c in range(FG)]
+        tensor_order = lead_in(turn_z, turn_x, scores, project) + [(mix, 0, e) for e in range(2)]
+
+        later_v = [(og, gj, s) for og in range(1, OG) for gj in range(NG) for s in range(PACK)]
+        filled_by_step = [0, 4, 8, 10, 12, 14, 16]
+        vector_before = {2: [(quant_v, 1, 0)], 3: [(quant_v, 1, 1)], 7: [(quant_v, 2, 1)]}
+        vector_after = {0: [(quant_w, 1, 1, 0, 2), (scale_a, 1, 1), (quant_w, 2, 0, 0, 2), (quant_a, 1, 1)],
+                        1: [(quant_w, 2, 1, 0, 2)], 5: [(quant_v, 2, 0)]}
+
+        def v_banks(step, k):
+            if not 0 <= k < len(filled_by_step) - 1:
+                return [], []
+            due = [(step, *key) for key in later_v[filled_by_step[k]:filled_by_step[k + 1]]]
+            return due[:2], due[2:]
+
+        last = PAIRS - 1
+        for k in range(last):
+            vector_order.extend(vector_before.get(k, []) + [(affine, k, e) for e in range(2)])
+            if k >= 1:
                 vector_order.append((finish, k - 1, 0, 2))
-            vector_order.extend(side_w.get(k, []))
-            if 0 <= k - 3 < steps and (k - 3) % 2 == 1:
-                vector_order.append((emit_planes, *unit(k - 3)[:2]))
-            scalar_order.extend(side_p.get(k, []))
-            if k < steps:
-                scalar_order.append((squash, k, 0, 2))
-            scalar_order.extend(side_q.get(k, []))
-            if 0 <= k - 1 < steps and eng == "s":
-                scalar_order.append((round_y, k - 1, 0, 2, eng))
-            scalar_order.extend(side_s.get(k, []))
-            if 0 <= k - 2 < steps:
-                scalar_order.append((drain_y, k - 2, 0, 2))
-            sb = [(project, *b) for b in side_b.get(k, [])]
-            if k + 1 < steps:
-                tensor_order.append((mix, k + 1, 0))
-            tensor_order.extend(sb[:2])
-            if 0 <= k - 2 < steps:
-                tensor_order.append((turn_y, k - 2, 0, 2))
-            if k + 1 < steps:
-                tensor_order.append((mix, k + 1, 1))
-            tensor_order.extend(sb[2:])
-        k = steps - 1
-        vector_order.extend([(affine, k, 0), (affine, k, 1), (finish, k - 1, 0, 2), (finish, k, 0, 1),
-                             (round_y, k - 1, 0, 2, "v"), (finish, k, 1, 2), (round_y, k, 0, 1, "v"), (emit_planes, 2, 0),
-                             (round_y, k, 1, 2, "v"), (emit_planes, 2, 1)])
-        scalar_order.extend([(squash, k, 0, 1), (squash, k, 1, 2), (drain_y, k - 2, 0, 2), (drain_y, k - 1, 0, 2),
-                             (drain_y, k, 0, 1), (drain_y, k, 1, 2)])
-        tensor_order.extend([(turn_y, k - 2, 0, 2), (turn_y, k - 1, 0, 2), (turn_y, k, 0, 1), (turn_y, k, 1, 2)])
-        steps = 2 * NG * OG
+            vector_order.extend(vector_after.get(k, []))
+            if k - 2 in ROUND_ON_VECTOR:
+                vector_order.append((round_y, k - 2, on_vector, 0, 2))
+            if k >= 4 and k % 2 == 1:
+                vector_order.append((emit_planes, *place_of(k - 4)[:2]))
+
+            early, late = v_banks(drain_v, k - 1)
+            scalar_order.extend(late or early)
+            scalar_order.append((squash, k, 0, 2))
+            if k >= 2 and k - 2 not in ROUND_ON_VECTOR:
+                scalar_order.append((round_y, k - 2, on_scalar, 0, 2))
+            early, late = v_banks(drain_v, k)
+            if late:
+                scalar_order.extend(early)
+            if k >= 3:
+                scalar_order.append((drain_y, k - 3, 0, 2))
+
+            early, late = v_banks(project, k)
+            tensor_order.extend([(mix, k + 1, 0)] + early + [(mix, k + 1, 1)])
+            if k >= 3:
+                tensor_order.append((turn_y, k - 3, 0, 2))
+            tensor_order.extend(late)
+
+        tiles = [(e, e + 1) for e in range(2)]
+        vector_order.extend(
+            [(affine, last, e) for e in range(2)]
+            + [(finish, last - 1, 0, 2), (emit_planes, *place_of(last - 4)[:2]), (round_y, last - 1, on_vector, 0, 2)]
+            + [(finish, last, *r) for r in tiles] + [(round_y, last, on_vector, *r) for r in tiles]
+            + [(emit_planes, OG - 1, gi) for gi in range(NG)])
+        turns = [(last - 3, 0, 2), (last - 1, 0, 2), (last - 2, 0, 2)] + [(last, *r) for r in tiles]
+        scalar_order.extend([(squash, last, *r) for r in tiles] + [(round_y, last - 2, on_scalar, 0, 2)]
+                            + [(drain_y, *key) for key in turns])
+        tensor_order.extend([(turn_y, *key) for key in turns])
+
+
+        def halves(step, key, lo, hi):
+            return [(step, *key, e) for e in range(lo, hi)]
+
         needs = {
             turn_z: lambda g, h: [],
             turn_x: lambda g, t: [],
-            weave_w: lambda og, c, on_vector: [],
+            weave_w: lambda og, c, copy, lo, hi: [],
             drain_z: lambda g, h: [(turn_z, g, h)],
             drain_x: lambda g, t: [(turn_x, g, t)],
-            scale_z: lambda g: [(drain_z, g, h) for h in range(2)],
-            quant_z: lambda g: [(drain_z, g, h) for h in range(2)],
-            quant_zr: lambda g: [(scale_z, g)],
-            quant_x: lambda g: [(drain_x, g, t) for t in range(PACK)],
-            quant_w: lambda og, c: [(weave_w, og, c)],
-            scores: lambda gj, gi, s: [(quant_zr, gj), (quant_z, gi)],
+            scale_z: lambda g, lo, hi: halves(drain_z, [g], lo, hi),
+            quant_z: lambda g, lo, hi: halves(drain_z, [g], lo, hi),
+            quant_zr: lambda g, lo, hi: halves(scale_z, [g], lo, hi),
+            quant_x: lambda g: quarters(drain_x, g),
+            quant_w: lambda og, c, lo, hi: halves(weave_w, [og, c], lo, hi),
+            scores: lambda gj, gi, s: halves(quant_zr, [gj], 0, 2) + [(quant_z, gi, s // 2)],
             sigmoid: lambda gj, gi, s: [(scores, gj, gi, s)],
-            scale_a: lambda gj, gi: [(sigmoid, gj, gi, s) for s in range(PACK)],
+            scale_a: lambda gj, gi: quarters(sigmoid, gj, gi),
             quant_a: lambda gj, gi: [(scale_a, gj, gi)],
-            project: lambda og, gj, s: [(quant_x, gj)] + [(quant_w, og, c) for c in range(FG)],
+            project: lambda og, gj, s: [(quant_x, gj)] + [(quant_w, og, c, s // 2) for c in range(FG)],
             drain_v: lambda og, gj, s: [(project, og, gj, s)],
-            quant_v: lambda og, gj: [(drain_v, og, gj, s) for s in range(PACK)],
-            mix: lambda k, e: [(f, *key) for gj in range(NG) for f, key in ((quant_a, (gj, unit(k)[1])), (quant_v, (unit(k)[0], gj)))],
+            quant_v: lambda og, gj: quarters(drain_v, og, gj),
+            mix: lambda k, e: ([(quant_a, gj, place_of(k)[1]) for gj in range(NG)]
+                               + [(quant_v, place_of(k)[0], gj) for gj in range(NG)]),
             affine: lambda k, e: [(mix, k, e)],
-            squash: lambda k, lo, hi: [(affine, k, e) for e in range(lo, hi)],
-            finish: lambda k, lo, hi: [(squash, k, e) for e in range(lo, hi)],
-            round_y: lambda k, lo, hi, engine: [(finish, k, e) for e in range(lo, hi)],
-            turn_y: lambda k, lo, hi: [(round_y, k, e) for e in range(lo, hi)],
-            drain_y: lambda k, lo, hi: [(turn_y, k, e) for e in range(lo, hi)],
+            squash: lambda k, lo, hi: halves(affine, [k], lo, hi),
+            finish: lambda k, lo, hi: halves(squash, [k], lo, hi),
+            round_y: lambda k, copy, lo, hi: halves(finish, [k], lo, hi),
+            turn_y: lambda k, lo, hi: halves(round_y, [k], lo, hi),
+            drain_y: lambda k, lo, hi: halves(turn_y, [k], lo, hi),
             emit_planes: lambda og, gi: [(drain_y, 2 * (NG * og + gi) + h, e) for h in range(2) for e in range(2)],
         }
-        opens = {turn_z: "wide", turn_x: "wide", mix: "wide", scores: "quad", project: "quad", turn_y: "quad"}
-        closes = {drain_z: "wide", drain_x: "wide", affine: "wide", sigmoid: "quad", drain_v: "quad", drain_y: "quad"}
-        free = {"wide": BANKS["wide"], "quad": BANKS["quad"], None: 1}
+        ranged = {scale_z: 1, quant_z: 1, quant_zr: 1, weave_w: 2, quant_w: 2,
+                  squash: 1, finish: 1, round_y: 1, turn_y: 1, drain_y: 1}
+        fills = {turn_z: "wide", turn_x: "wide", mix: "wide", scores: "quad", project: "quad", turn_y: "quad"}
+        empties = {drain_z: "wide", drain_x: "wide", affine: "wide", sigmoid: "quad", drain_v: "quad", drain_y: "quad"}
+        free = dict(BANKS)
         done = set()
-        queues = [vector_order, scalar_order, tensor_order, pool_order]
-        place = [0, 0, 0, 0]
-        while any(place[q] < len(queues[q]) for q in range(4)):
-            moved = False
-            for q in range(4):
-                if place[q] == len(queues[q]):
+        orders = [vector_order, scalar_order, tensor_order]
+        written = [0, 0, 0]
+        while any(written[q] < len(order) for q, order in enumerate(orders)):
+            before = sum(written)
+            for q, order in enumerate(orders):
+                if written[q] == len(order):
                     continue
-                step = queues[q][place[q]]
-                f, key = step[0], step[1:]
-                if all(n in done for n in needs[f](*key)) and free[opens.get(f)] > 0:
-                    f(*key)
-                    if f in (squash, finish, round_y, turn_y, drain_y):
-                        for e in range(key[1], key[2]):
-                            done.add((f, key[0], e))
-                    else:
-                        done.add(step[:-1] if f == weave_w else step)
-                    if f in opens:
-                        free[opens[f]] = free[opens[f]] - 1
-                    if f in closes:
-                        free[closes[f]] = free[closes[f]] + 1
-                    place[q] = place[q] + 1
-                    moved = True
-            assert moved
+                step, key = order[written[q]][0], order[written[q]][1:]
+                if any(n not in done for n in needs[step](*key)) or (step in fills and free[fills[step]] == 0):
+                    continue
+                step(*key)
+                for part in halves(step, key[:ranged[step]], *key[-2:]) if step in ranged else [(step, *key)]:
+                    done.add(part)
+                if step in fills:
+                    free[fills[step]] = free[fills[step]] - 1
+                if step in empties:
+                    free[empties[step]] = free[empties[step]] + 1
+                written[q] = written[q] + 1
+            assert sum(written) > before

@@ -86,26 +86,29 @@ def tile_distmult_sigmoid_neighbour_mix_h3_kernel(
             nc.sync.dma_start(out=x_raw[g, h][:], in_=rows[:, 2 * h * F:2 * (h + 1) * F])
 
         def load_w(og, c, lo, hi):
-            w_raw[og, c, lo] = work.tile([P, PACK, (hi - lo) * H], BF16, name="w_raw", tag="w_raw", bufs=5)
-            block = w[c * G:(c + 1) * G, og * G + lo * H:og * G + hi * H]
-            nc.sync.dma_start(out=w_raw[og, c, lo][:], in_=block.rearrange("(p t) o -> p t o", t=PACK))
+            if og == 0:
+                raw = keep.tile([P, PACK, (hi - lo) * P], BF16, name="w_first%d%d" % (c, lo))
+            else:
+                raw = work.tile([P, PACK, (hi - lo) * P], BF16, name="w_raw", tag="w_raw", bufs=3)
+            for s in range(lo, hi):
+                w_raw[og, c, s] = raw, lo
+            block = w[c * G:(c + 1) * G, og * G + lo * P:og * G + hi * P]
+            nc.sync.dma_start(out=raw[:], in_=block.rearrange("(p t) o -> p t o", t=PACK))
 
-        for h in range(2):
-            load_w(0, 0, h, h + 1)
-            load_z(0, h)
-        for h in range(2):
-            load_z(1, h)
-        for h in range(2):
-            load_x(0, h)
-        load_w(0, 1, 0, 2)
-        for h in range(2):
-            load_x(1, h)
+        for g in range(NG):
+            for h in range(2):
+                load_w(0, g, 2 * h, 2 * h + 2)
+                load_z(g, h)
+        for g in range(NG):
+            for h in range(2):
+                load_x(g, h)
         for c in range(FG):
-            load_w(1, c, 0, 2)
+            load_w(1, c, 0, PACK)
         bias_sb = keep.tile([P, O], BF16, name="bias_sb")
         gain_sb = keep.tile([P, O], BF16, name="gain_sb")
         nc.sync.dma_start(out=bias_sb[:], in_=bias.partition_broadcast(P))
         nc.sync.dma_start(out=gain_sb[:], in_=gain.partition_broadcast(P))
+        load_w(2, 0, 0, PACK)
 
         z_mx = [mx_operand("z%d" % g, G) for g in range(NG)]
         zr_mx = [mx_operand("zr%d" % g, G) for g in range(NG)]
@@ -167,15 +170,16 @@ def tile_distmult_sigmoid_neighbour_mix_h3_kernel(
             quantize(cols(x_mx[g], 0, FG * G), xt[g][:])
 
         def weave_w(og, c, copy, lo, hi):
-            if lo == 0:
-                wt[og, c] = woven("wt", bufs=3)
-            copy(out=wt[og, c][:, lo * H * PACK:hi * H * PACK].rearrange("p (a i t) -> p a t i", i=4, t=PACK),
-                 in_=w_raw[og, c, lo][:].rearrange("p t (a i) -> p a t i", i=4))
-            if og == 0 and hi == 2:
-                load_w(OG - 1, c, 0, 2)
+            if (og, c) not in wt:
+                wt[og, c] = woven("wt")
+            raw, first = w_raw[og, c, lo]
+            copy(out=wt[og, c][:, lo * G:hi * G].rearrange("p (a i t) -> p a t i", i=4, t=PACK),
+                 in_=raw[:, :, (lo - first) * P:(hi - first) * P].rearrange("p t (a i) -> p a t i", i=4))
+            if (og, c) == (1, 0):
+                load_w(2, 1, 0, PACK)
 
         def quant_w(og, c, lo, hi):
-            quantize(cols(w_mx[og, c], lo * H, (hi - lo) * H), wt[og, c][:, lo * H * PACK:hi * H * PACK])
+            quantize(cols(w_mx[og, c], lo * P, (hi - lo) * P), wt[og, c][:, lo * G:hi * G])
 
         def scores(gj, gi, s):
             ps = banks["p", gj, gi, s] = bank("quad")
@@ -246,7 +250,7 @@ def tile_distmult_sigmoid_neighbour_mix_h3_kernel(
             nc.sync.dma_start(out=rows[:, 2 * h + lo:2 * h + hi, :], in_=yf[k][:, lo:hi, :])
 
         def round_y(k, copy, lo, hi):
-            ys[k, lo] = work.tile([P, (hi - lo) * G], BF16, name="ys", tag="ys", bufs=3)
+            ys[k, lo] = work.tile([P, (hi - lo) * G], BF16, name="ys", tag="ys", bufs=4)
             copy(out=ys[k, lo][:].rearrange("m (u n b) -> m u n b", u=2, b=2),
                  in_=yf[k][:, lo:hi, :].rearrange("m e (p u b) -> m u (e p) b", u=2, b=2))
 
@@ -288,23 +292,25 @@ def tile_distmult_sigmoid_neighbour_mix_h3_kernel(
             return order + quarters(v_step, 0, 0) + quarters(v_step, 0, 1) + ps[12:]
 
         vector_order = [
-            (weave_w, 0, 0, on_vector, 0, 1), (quant_w, 0, 0, 0, 1), (weave_w, 0, 0, on_vector, 1, 2),
-            (scale_z, 0, 0, 1), (quant_w, 0, 0, 1, 2), (quant_z, 0, 0, 1), (quant_zr, 0, 0, 1),
-            (scale_z, 0, 1, 2), (quant_z, 0, 1, 2), (quant_zr, 0, 1, 2),
-            (scale_z, 1, 0, 2), (quant_z, 1, 0, 2), (quant_zr, 1, 0, 2),
-            (weave_w, 0, 1, on_vector, 0, 2), (scale_a, 0, 0), (quant_w, 0, 1, 0, 2), (quant_x, 0), (quant_a, 0, 0),
-            (scale_a, 1, 0), (quant_x, 1), (quant_a, 1, 0),
-            (weave_w, 1, 0, on_vector, 0, 2), (quant_v, 0, 0), (quant_w, 1, 0, 0, 2),
-            (scale_a, 0, 1), (quant_v, 0, 1), (quant_a, 0, 1), (weave_w, 1, 1, on_vector, 0, 2),
+            (weave_w, 0, 0, on_vector, 0, 2), (quant_w, 0, 0, 0, 2), (weave_w, 0, 0, on_vector, 2, 4), (quant_w, 0, 0, 2, 4),
+            (scale_z, 0, 0, 1), (quant_z, 0, 0, 1), (quant_zr, 0, 0, 1),
+            (scale_z, 0, 1, 2), (quant_z, 0, 1, 2), (quant_zr, 0, 1, 2), (quant_w, 0, 1, 0, 2),
+            (scale_z, 1, 0, 2), (quant_z, 1, 0, 2), (quant_zr, 1, 0, 2), (quant_w, 0, 1, 2, 4),
+            (scale_a, 0, 0), (weave_w, 1, 0, on_vector, 0, 4), (quant_x, 0), (quant_a, 0, 0),
+            (scale_a, 1, 0), (quant_w, 1, 0, 0, 4), (quant_x, 1), (quant_a, 1, 0),
+            (weave_w, 1, 1, on_vector, 0, 4), (quant_v, 0, 0), (quant_w, 1, 1, 0, 4),
+            (scale_a, 0, 1), (quant_v, 0, 1), (quant_a, 0, 1), (weave_w, 2, 1, on_vector, 2, 4),
         ]
-        scalar_order = lead_in(drain_z, drain_x, sigmoid, drain_v) + [(weave_w, OG - 1, c, on_scalar, 0, 2) for c in range(FG)]
+        scalar_banks = lead_in(drain_z, drain_x, sigmoid, drain_v)
+        scalar_order = ([s for n in range(PACK) for s in (scalar_banks[n], (weave_w, 0, 1, on_scalar, n, n + 1))]
+                        + scalar_banks[PACK:] + [(weave_w, 2, 0, on_scalar, 0, 4), (weave_w, 2, 1, on_scalar, 0, 2)])
         tensor_order = lead_in(turn_z, turn_x, scores, project) + [(mix, 0, e) for e in range(2)]
 
         later_v = [(og, gj, s) for og in range(1, OG) for gj in range(NG) for s in range(PACK)]
         filled_by_step = [0, 4, 8, 10, 12, 14, 16]
         vector_before = {2: [(quant_v, 1, 0)], 3: [(quant_v, 1, 1)], 7: [(quant_v, 2, 1)]}
-        vector_after = {0: [(quant_w, 1, 1, 0, 2), (scale_a, 1, 1), (quant_w, 2, 0, 0, 2), (quant_a, 1, 1)],
-                        1: [(quant_w, 2, 1, 0, 2)], 5: [(quant_v, 2, 0)]}
+        vector_after = {0: [(scale_a, 1, 1), (quant_w, 2, 0, 0, 4), (quant_a, 1, 1)],
+                        1: [(quant_w, 2, 1, 0, 4)], 5: [(quant_v, 2, 0)]}
 
         def v_banks(step, k):
             if not 0 <= k < len(filled_by_step) - 1:
@@ -352,7 +358,7 @@ def tile_distmult_sigmoid_neighbour_mix_h3_kernel(
         tensor_order.extend([(turn_y, *key) for key in turns])
 
 
-        def halves(step, key, lo, hi):
+        def parts(step, key, lo, hi):
             return [(step, *key, e) for e in range(lo, hi)]
 
         needs = {
@@ -361,26 +367,26 @@ def tile_distmult_sigmoid_neighbour_mix_h3_kernel(
             weave_w: lambda og, c, copy, lo, hi: [],
             drain_z: lambda g, h: [(turn_z, g, h)],
             drain_x: lambda g, t: [(turn_x, g, t)],
-            scale_z: lambda g, lo, hi: halves(drain_z, [g], lo, hi),
-            quant_z: lambda g, lo, hi: halves(drain_z, [g], lo, hi),
-            quant_zr: lambda g, lo, hi: halves(scale_z, [g], lo, hi),
+            scale_z: lambda g, lo, hi: parts(drain_z, [g], lo, hi),
+            quant_z: lambda g, lo, hi: parts(drain_z, [g], lo, hi),
+            quant_zr: lambda g, lo, hi: parts(scale_z, [g], lo, hi),
             quant_x: lambda g: quarters(drain_x, g),
-            quant_w: lambda og, c, lo, hi: halves(weave_w, [og, c], lo, hi),
-            scores: lambda gj, gi, s: halves(quant_zr, [gj], 0, 2) + [(quant_z, gi, s // 2)],
+            quant_w: lambda og, c, lo, hi: parts(weave_w, [og, c], lo, hi),
+            scores: lambda gj, gi, s: parts(quant_zr, [gj], 0, 2) + [(quant_z, gi, s // 2)],
             sigmoid: lambda gj, gi, s: [(scores, gj, gi, s)],
             scale_a: lambda gj, gi: quarters(sigmoid, gj, gi),
             quant_a: lambda gj, gi: [(scale_a, gj, gi)],
-            project: lambda og, gj, s: [(quant_x, gj)] + [(quant_w, og, c, s // 2) for c in range(FG)],
+            project: lambda og, gj, s: [(quant_x, gj)] + [(quant_w, og, c, s) for c in range(FG)],
             drain_v: lambda og, gj, s: [(project, og, gj, s)],
             quant_v: lambda og, gj: quarters(drain_v, og, gj),
             mix: lambda k, e: ([(quant_a, gj, place_of(k)[1]) for gj in range(NG)]
                                + [(quant_v, place_of(k)[0], gj) for gj in range(NG)]),
             affine: lambda k, e: [(mix, k, e)],
-            squash: lambda k, lo, hi: halves(affine, [k], lo, hi),
-            finish: lambda k, lo, hi: halves(squash, [k], lo, hi),
-            round_y: lambda k, copy, lo, hi: halves(finish, [k], lo, hi),
-            turn_y: lambda k, lo, hi: halves(round_y, [k], lo, hi),
-            drain_y: lambda k, lo, hi: halves(turn_y, [k], lo, hi),
+            squash: lambda k, lo, hi: parts(affine, [k], lo, hi),
+            finish: lambda k, lo, hi: parts(squash, [k], lo, hi),
+            round_y: lambda k, copy, lo, hi: parts(finish, [k], lo, hi),
+            turn_y: lambda k, lo, hi: parts(round_y, [k], lo, hi),
+            drain_y: lambda k, lo, hi: parts(turn_y, [k], lo, hi),
             emit_planes: lambda og, gi: [(drain_y, 2 * (NG * og + gi) + h, e) for h in range(2) for e in range(2)],
         }
         ranged = {scale_z: 1, quant_z: 1, quant_zr: 1, weave_w: 2, quant_w: 2,
@@ -400,7 +406,7 @@ def tile_distmult_sigmoid_neighbour_mix_h3_kernel(
                 if any(n not in done for n in needs[step](*key)) or (step in fills and free[fills[step]] == 0):
                     continue
                 step(*key)
-                for part in halves(step, key[:ranged[step]], *key[-2:]) if step in ranged else [(step, *key)]:
+                for part in parts(step, key[:ranged[step]], *key[-2:]) if step in ranged else [(step, *key)]:
                     done.add(part)
                 if step in fills:
                     free[fills[step]] = free[fills[step]] - 1

@@ -67,8 +67,6 @@ def tile_distmult_sigmoid_neighbour_mix_h3_kernel(
         send_sb = keep.tile([P, NG, PACK], BF16, name="send_sb")
         recv_sb = keep.tile([P, NG, PACK], BF16, name="recv_sb")
         nc.scalar.dma_start(out=rel_sb[:], in_=relation.rearrange("(p t) -> p t", t=PACK))
-        nc.scalar.dma_start(out=send_sb[:], in_=send.rearrange("(g p t) -> p g t", g=NG, t=PACK))
-        nc.scalar.dma_start(out=recv_sb[:], in_=recv.rearrange("(g p t) -> p g t", g=NG, t=PACK))
 
         warm = keep.tile([P, 1], F32, name="warm")
         nc.scalar.activation(out=warm[:], in_=ident[:, 0:1], func=ACT.Sigmoid)
@@ -99,11 +97,13 @@ def tile_distmult_sigmoid_neighbour_mix_h3_kernel(
             for h in range(2):
                 load_w(0, g, 2 * h, 2 * h + 2)
                 load_z(g, h)
+        nc.sync.dma_start(out=send_sb[:], in_=send.rearrange("(g p t) -> p g t", g=NG, t=PACK))
         for g in range(NG):
             for h in range(2):
                 load_x(g, h)
         for c in range(FG):
             load_w(1, c, 0, PACK)
+        nc.sync.dma_start(out=recv_sb[:], in_=recv.rearrange("(g p t) -> p g t", g=NG, t=PACK))
         bias_sb = keep.tile([P, O], BF16, name="bias_sb")
         gain_sb = keep.tile([P, O], BF16, name="gain_sb")
         nc.sync.dma_start(out=bias_sb[:], in_=bias.partition_broadcast(P))
@@ -294,7 +294,8 @@ def tile_distmult_sigmoid_neighbour_mix_h3_kernel(
         vector_order = [
             (weave_w, 0, 0, on_vector, 0, 2), (quant_w, 0, 0, 0, 2), (weave_w, 0, 0, on_vector, 2, 4), (quant_w, 0, 0, 2, 4),
             (scale_z, 0, 0, 1), (quant_z, 0, 0, 1), (quant_zr, 0, 0, 1),
-            (scale_z, 0, 1, 2), (quant_z, 0, 1, 2), (quant_zr, 0, 1, 2), (quant_w, 0, 1, 0, 2),
+            (scale_z, 0, 1, 2), (quant_z, 0, 1, 2), (quant_zr, 0, 1, 2),
+            (weave_w, 0, 1, on_vector, 2, 4), (quant_w, 0, 1, 0, 2),
             (scale_z, 1, 0, 2), (quant_z, 1, 0, 2), (quant_zr, 1, 0, 2), (quant_w, 0, 1, 2, 4),
             (scale_a, 0, 0), (weave_w, 1, 0, on_vector, 0, 4), (quant_x, 0), (quant_a, 0, 0),
             (scale_a, 1, 0), (quant_w, 1, 0, 0, 4), (quant_x, 1), (quant_a, 1, 0),
@@ -302,8 +303,8 @@ def tile_distmult_sigmoid_neighbour_mix_h3_kernel(
             (scale_a, 0, 1), (quant_v, 0, 1), (quant_a, 0, 1), (weave_w, 2, 1, on_vector, 2, 4),
         ]
         scalar_banks = lead_in(drain_z, drain_x, sigmoid, drain_v)
-        scalar_order = ([s for n in range(PACK) for s in (scalar_banks[n], (weave_w, 0, 1, on_scalar, n, n + 1))]
-                        + scalar_banks[PACK:] + [(weave_w, 2, 0, on_scalar, 0, 4), (weave_w, 2, 1, on_scalar, 0, 2)])
+        scalar_order = ([s for n in range(2) for s in (scalar_banks[n], (weave_w, 0, 1, on_scalar, n, n + 1))]
+                        + scalar_banks[2:] + [(weave_w, 2, 0, on_scalar, 0, 4), (weave_w, 2, 1, on_scalar, 0, 2)])
         tensor_order = lead_in(turn_z, turn_x, scores, project) + [(mix, 0, e) for e in range(2)]
 
         later_v = [(og, gj, s) for og in range(1, OG) for gj in range(NG) for s in range(PACK)]

from contextlib import ExitStack

import concourse.mybir as mybir
from concourse.masks import make_identity

NODES, D, F, O = 1024, 512, 1024, 1536
FLOPS = 2 * NODES * NODES * D + 2 * NODES * F * O + 2 * NODES * NODES * O

F32 = mybir.dt.float32
BF16 = mybir.dt.bfloat16
U32 = mybir.dt.uint32
I32 = mybir.dt.int32
U8 = mybir.dt.uint8
FP8X4 = mybir.dt.float8_e4m3fn_x4
ACT = mybir.ActivationFunctionType
ALU = mybir.AluOpType

P = 128
PACK = 4
G = P * PACK
H = G // 2
NG = NODES // G
FG = F // G
OG = O // G
PAIRS = 2 * NG * OG

BANKS = {"wide": 3, "quad": 5}
ROUND_ON_VECTOR = range(1, 4)


def tile_distmult_sigmoid_neighbour_mix_h3_kernel(
    tc, z, relation, x, w, send, recv, bias, gain, out_0, out_1, out_2
):
    nc = tc.nc
    with ExitStack() as ctx:
        keep = ctx.enter_context(tc.tile_pool(name="keep", bufs=1))
        work = ctx.enter_context(tc.tile_pool(name="work", bufs=2))
        psum = ctx.enter_context(tc.psum_pool(name="psum", bufs=1))
        ctx.enter_context(tc.manual_schedule())
        on_vector, on_scalar = nc.vector.tensor_copy, nc.scalar.copy

        def bank(tag):
            return psum.tile([P, G], F32, name=tag, tag=tag, bufs=BANKS[tag])

        def woven(tag, bufs=2, groups=1):
            return work.tile([P, groups * G * PACK], BF16, name=tag, tag=tag, bufs=bufs, align_bytes=64)

        def mx_operand(name, width):
            codes = keep.tile([P, width], U32, name=name + "_codes", align_bytes=64)
            scales = keep.tile([P, width], U8, name=name + "_scales", align_bytes=64)
            return codes, scales

        def cols(operand, first, n):
            return operand[0][:, first:first + n], operand[1][:, first:first + n]

        def quantize(operand, src):
            nc.vector.quantize_mx(out=operand[0].bitcast(FP8X4), scales=operand[1], in_=src)

        def matmul(out, stationary, moving, start, stop):
            nc.tensor.matmul_mx(out=out, lhsT=stationary[0].bitcast(FP8X4), lhsT_scale=stationary[1],
                                rhs=moving[0].bitcast(FP8X4), rhs_scale=moving[1], start=start, stop=stop)

        ident = keep.tile([P, P], F32, name="ident")
        make_identity(nc, ident[:])

        rel_sb = keep.tile([P, PACK], BF16, name="rel_sb")
        send_sb = keep.tile([P, NG, PACK], BF16, name="send_sb")
        recv_sb = keep.tile([P, NG, PACK], BF16, name="recv_sb")
        nc.scalar.dma_start(out=rel_sb[:], in_=relation.rearrange("(p t) -> p t", t=PACK))

        warm = keep.tile([P, 1], F32, name="warm")
        nc.scalar.activation(out=warm[:], in_=ident[:, 0:1], func=ACT.Sigmoid)

        z_raw, x_raw, w_raw = {}, {}, {}

        def load_z(g, h):
            z_raw[g, h] = keep.tile([P, 2 * D], BF16, name="z_raw%d%d" % (g, h))
            rows = z[g * G:(g + 1) * G, :].rearrange("(m t) d -> m (t d)", t=PACK)
            nc.sync.dma_start(out=z_raw[g, h][:], in_=rows[:, 2 * h * D:2 * (h + 1) * D])

        def load_x(g, h):
            x_raw[g, h] = keep.tile([P, 2 * F], BF16, name="x_raw%d%d" % (g, h))
            rows = x[g * G:(g + 1) * G, :].rearrange("(m t) f -> m (t f)", t=PACK)
            nc.sync.dma_start(out=x_raw[g, h][:], in_=rows[:, 2 * h * F:2 * (h + 1) * F])

        def load_w(og, c, lo, hi):
            if og == 0:
                raw = keep.tile([P, PACK, (hi - lo) * P], BF16, name="w_first%d%d" % (c, lo))
            else:
                raw = work.tile([P, PACK, (hi - lo) * P], BF16, name="w_raw", tag="w_raw", bufs=3)
            for s in range(lo, hi):
                w_raw[og, c, s] = raw, lo
            block = w[c * G:(c + 1) * G, og * G + lo * P:og * G + hi * P]
            nc.sync.dma_start(out=raw[:], in_=block.rearrange("(p t) o -> p t o", t=PACK))

        for g in range(NG):
            for h in range(2):
                load_w(0, g, 2 * h, 2 * h + 2)
                load_z(g, h)
        nc.sync.dma_start(out=send_sb[:], in_=send.rearrange("(g p t) -> p g t", g=NG, t=PACK))
        for g in range(NG):
            for h in range(2):
                load_x(g, h)
        for c in range(FG):
            load_w(1, c, 0, PACK)
        nc.sync.dma_start(out=recv_sb[:], in_=recv.rearrange("(g p t) -> p g t", g=NG, t=PACK))
        bias_sb = keep.tile([P, O], BF16, name="bias_sb")
        gain_sb = keep.tile([P, O], BF16, name="gain_sb")
        nc.sync.dma_start(out=bias_sb[:], in_=bias.partition_broadcast(P))
        nc.sync.dma_start(out=gain_sb[:], in_=gain.partition_broadcast(P))
        load_w(2, 0, 0, PACK)

        z_mx = [mx_operand("z%d" % g, G) for g in range(NG)]
        zr_mx = [mx_operand("zr%d" % g, G) for g in range(NG)]
        x_mx = [mx_operand("x%d" % g, FG * G) for g in range(NG)]
        w_mx = {(og, c): mx_operand("w%d%d" % (og, c), G) for og in range(OG) for c in range(FG)}
        a_mx = {(gj, gi): mx_operand("a%d%d" % (gj, gi), G) for gj in range(NG) for gi in range(NG)}
        v_mx = {(og, gj): mx_operand("v%d%d" % (og, gj), G) for og in range(OG) for gj in range(NG)}
        y_scales = [keep.tile([P, NODES], U8, name="y_scales%d" % og, align_bytes=64) for og in range(OG)]

        banks = {}
        zt, zrt, xt, wt, sig, at, vt, pre, yf, ys, yt = {}, {}, {}, {}, {}, {}, {}, {}, {}, {}, {}


        def turn_z(g, h):
            ps = banks["z", g, h] = bank("wide")
            words = z_raw[g, h][:].bitcast(F32)
            for t in range(2):
                for u in range(2):
                    q = 2 * t + u
                    nc.tensor.transpose(ps[:, q * P:(q + 1) * P], words[:, t * H + u:(t + 1) * H:2], ident[:])

        def drain_z(g, h):
            if h == 0:
                zt[g] = woven("zt")
            dst = zt[g][:].bitcast(F32)[:, h * G:(h + 1) * G]
            nc.scalar.copy(out=dst.rearrange("p (t m u) -> p t m u", t=2, u=2),
                           in_=banks["z", g, h][:].rearrange("p (t u m) -> p t m u", t=2, u=2))

        def scale_z(g, lo, hi):
            if lo == 0:
                zrt[g] = woven("zrt", bufs=1)
            part = slice(lo * H * PACK, hi * H * PACK)
            nc.vector.tensor_tensor(out=zrt[g][:, part].rearrange("p (n t) -> p n t", t=PACK),
                                    in0=zt[g][:, part].rearrange("p (n t) -> p n t", t=PACK),
                                    in1=rel_sb[:].unsqueeze(1).to_broadcast([P, (hi - lo) * H, PACK]), op=ALU.mult)

        def quant_z(g, lo, hi):
            quantize(cols(z_mx[g], lo * H, (hi - lo) * H), zt[g][:, lo * H * PACK:hi * H * PACK])

        def quant_zr(g, lo, hi):
            quantize(cols(zr_mx[g], lo * H, (hi - lo) * H), zrt[g][:, lo * H * PACK:hi * H * PACK])

        def turn_x(g, t):
            ps = banks["x", g, t] = bank("wide")
            words = x_raw[g, t // 2][:].bitcast(F32)
            for c in range(FG):
                for u in range(2):
                    q = 2 * c + u
                    first = ((t % 2) * FG + c) * H
                    nc.tensor.transpose(ps[:, q * P:(q + 1) * P], words[:, first + u:first + H:2], ident[:])

        def drain_x(g, t):
            if t == 0:
                xt[g] = woven("xt", groups=FG)
            dst = xt[g][:].bitcast(F32).rearrange("p (c t m u) -> p c t m u", c=FG, t=PACK, u=2)[:, :, t, :, :]
            nc.scalar.copy(out=dst, in_=banks["x", g, t][:].rearrange("p (c u m) -> p c m u", c=FG, u=2))

        def quant_x(g):
            quantize(cols(x_mx[g], 0, FG * G), xt[g][:])

        def weave_w(og, c, copy, lo, hi):
            if (og, c) not in wt:
                wt[og, c] = woven("wt")
            raw, first = w_raw[og, c, lo]
            copy(out=wt[og, c][:, lo * G:hi * G].rearrange("p (a i t) -> p a t i", i=4, t=PACK),
                 in_=raw[:, :, (lo - first) * P:(hi - first) * P].rearrange("p t (a i) -> p a t i", i=4))
            if (og, c) == (1, 0):
                load_w(2, 1, 0, PACK)

        def quant_w(og, c, lo, hi):
            quantize(cols(w_mx[og, c], lo * P, (hi - lo) * P), wt[og, c][:, lo * G:hi * G])

        def scores(gj, gi, s):
            ps = banks["p", gj, gi, s] = bank("quad")
            for t in range(PACK):
                matmul(ps[:, t * P:(t + 1) * P], cols(zr_mx[gj], t * P, P), cols(z_mx[gi], s * P, P), True, True)

        def sigmoid(gj, gi, s):
            if s == 0:
                sig[gj, gi] = work.tile([P, G * PACK], F32, name="sig", tag="sig")
            nc.scalar.activation(out=sig[gj, gi][:, s * G:(s + 1) * G].rearrange("p (n t) -> p n t", t=PACK),
                                 in_=banks["p", gj, gi, s][:].rearrange("p (t n) -> p n t", t=PACK), func=ACT.Sigmoid)

        def scale_a(gj, gi):
            at[gj, gi] = woven("at")
            nc.vector.tensor_tensor(out=at[gj, gi][:].rearrange("p (n t) -> p n t", t=PACK),
                                    in0=sig[gj, gi][:].rearrange("p (n t) -> p n t", t=PACK),
                                    in1=send_sb[:, gj, :].unsqueeze(1).to_broadcast([P, G, PACK]), op=ALU.mult)

        def quant_a(gj, gi):
            quantize(cols(a_mx[gj, gi], 0, G), at[gj, gi][:])

        def project(og, gj, s):
            ps = banks["v", og, gj, s] = bank("quad")
            for t in range(PACK):
                for c in range(FG):
                    matmul(ps[:, t * P:(t + 1) * P], cols(x_mx[gj], c * G + t * P, P), cols(w_mx[og, c], s * P, P),
                           c == 0, c == FG - 1)

        def drain_v(og, gj, s):
            if s == 0:
                vt[og, gj] = woven("vt")
            nc.scalar.copy(out=vt[og, gj][:, s * G:(s + 1) * G].rearrange("p (n t) -> p n t", t=PACK),
                           in_=banks["v", og, gj, s][:].rearrange("p (t n) -> p n t", t=PACK))

        def quant_v(og, gj):
            quantize(cols(v_mx[og, gj], 0, G), vt[og, gj][:])

        def place_of(k):
            return k // (2 * NG), (k // 2) % NG, k % 2

        def mix(k, e):
            og, gi, h = place_of(k)
            ps = banks["s", k, e] = bank("wide")
            for gj in range(NG):
                matmul(ps[:], cols(a_mx[gj, gi], (2 * h + e) * P, P), cols(v_mx[og, gj], 0, G), gj == 0, gj == NG - 1)

        def affine(k, e):
            og, gi, h = place_of(k)
            if e == 0:
                pre[k] = work.tile([P, 2 * G], F32, name="pre", tag="pre", bufs=4)
            t = 2 * h + e
            nc.vector.scalar_tensor_tensor(out=pre[k][:, e * G:(e + 1) * G], in0=banks["s", k, e][:],
                                           scalar=recv_sb[:, gi, t:t + 1], in1=bias_sb[:, og * G:(og + 1) * G],
                                           op0=ALU.mult, op1=ALU.add)

        def squash(k, lo, hi):
            nc.scalar.activation(out=pre[k][:, lo * G:hi * G], in_=pre[k][:, lo * G:hi * G], func=ACT.Tanh)

        def finish(k, lo, hi):
            og, gi, h = place_of(k)
            if lo == 0:
                yf[k] = work.tile([P, 2, G], F32, name="yf", tag="yf", bufs=4)
            nc.vector.tensor_tensor(out=yf[k][:, lo:hi, :],
                                    in0=pre[k][:].rearrange("p (e o) -> p e o", e=2)[:, lo:hi, :],
                                    in1=gain_sb[:, og * G:(og + 1) * G].unsqueeze(1).to_broadcast([P, hi - lo, G]),
                                    op=ALU.mult)
            rows = out_0[gi * G:(gi + 1) * G, og * G:(og + 1) * G].rearrange("(m t) o -> m t o", t=PACK)
            nc.sync.dma_start(out=rows[:, 2 * h + lo:2 * h + hi, :], in_=yf[k][:, lo:hi, :])

        def round_y(k, copy, lo, hi):
            ys[k, lo] = work.tile([P, (hi - lo) * G], BF16, name="ys", tag="ys", bufs=4)
            copy(out=ys[k, lo][:].rearrange("m (u n b) -> m u n b", u=2, b=2),
                 in_=yf[k][:, lo:hi, :].rearrange("m e (p u b) -> m u (e p) b", u=2, b=2))

        def turn_y(k, lo, hi):
            ps = banks["y", k, lo] = bank("quad")
            words = ys[k, lo][:].bitcast(F32)
            for q in range(2 * (hi - lo)):
                nc.tensor.transpose(ps[:, q * P:(q + 1) * P], words[:, q * P:(q + 1) * P], ident[:])

        def drain_y(k, lo, hi):
            og, gi, h = place_of(k)
            if (og, gi) not in yt:
                yt[og, gi] = woven("yt")
            dst = yt[og, gi][:].bitcast(F32).rearrange("p (m t u) -> p m t u", t=PACK, u=2)
            src = banks["y", k, lo][:, :2 * (hi - lo) * P].rearrange("p (u e m) -> p m e u", u=2, m=P)
            nc.scalar.copy(out=dst[:, :, 2 * h + lo:2 * h + hi, :], in_=src)

        def emit_planes(og, gi):
            codes = work.tile([P, G], U32, name="y_codes", tag="y_codes", bufs=3, align_bytes=64)
            quantize((codes[:], y_scales[og][:, gi * G:(gi + 1) * G]), yt[og, gi][:])
            words = out_1[og].rearrange("p m t -> p (m t)").bitcast(I32)
            nc.sync.dma_start(out=words[:, gi * G:(gi + 1) * G], in_=codes[:].bitcast(I32))
            if gi == NG - 1:
                queue = nc.scalar if og == OG - 1 else nc.sync
                for q in range(4):
                    queue.dma_start(out=out_2[og, 4 * q:4 * q + 4, :].bitcast(I32),
                                    in_=y_scales[og][32 * q:32 * q + 4, :].bitcast(I32))


        def quarters(step, *key):
            return [(step, *key, s) for s in range(PACK)]

        def lead_in(z_step, x_step, p_step, v_step):
            xs = quarters(x_step, 0) + quarters(x_step, 1)
            ps = [s for gi in range(NG) for gj in range(NG) for s in quarters(p_step, gj, gi)]
            order = [(z_step, g, h) for g in range(NG) for h in range(2)] + ps[:4]
            for n in range(4):
                order = order + xs[2 * n:2 * n + 2] + ps[4 + 2 * n:6 + 2 * n]
            return order + quarters(v_step, 0, 0) + quarters(v_step, 0, 1) + ps[12:]

        vector_order = [
            (weave_w, 0, 0, on_vector, 0, 2), (quant_w, 0, 0, 0, 2), (weave_w, 0, 0, on_vector, 2, 4), (quant_w, 0, 0, 2, 4),
            (scale_z, 0, 0, 1), (quant_z, 0, 0, 1), (quant_zr, 0, 0, 1),
            (scale_z, 0, 1, 2), (quant_z, 0, 1, 2), (quant_zr, 0, 1, 2),
            (weave_w, 0, 1, on_vector, 2, 4), (quant_w, 0, 1, 0, 2),
            (scale_z, 1, 0, 2), (quant_z, 1, 0, 2), (quant_zr, 1, 0, 2), (quant_w, 0, 1, 2, 4),
            (scale_a, 0, 0), (weave_w, 1, 0, on_vector, 0, 4), (quant_x, 0), (quant_a, 0, 0),
            (scale_a, 1, 0), (quant_w, 1, 0, 0, 4), (quant_x, 1), (quant_a, 1, 0),
            (weave_w, 1, 1, on_vector, 0, 4), (quant_v, 0, 0), (quant_w, 1, 1, 0, 4),
            (scale_a, 0, 1), (quant_v, 0, 1), (quant_a, 0, 1), (weave_w, 2, 1, on_vector, 2, 4),
        ]
        scalar_banks = lead_in(drain_z, drain_x, sigmoid, drain_v)
        scalar_order = ([s for n in range(2) for s in (scalar_banks[n], (weave_w, 0, 1, on_scalar, n, n + 1))]
                        + scalar_banks[2:] + [(weave_w, 2, 0, on_scalar, 0, 4), (weave_w, 2, 1, on_scalar, 0, 2)])
        tensor_order = lead_in(turn_z, turn_x, scores, project) + [(mix, 0, e) for e in range(2)]

        later_v = [(og, gj, s) for og in range(1, OG) for gj in range(NG) for s in range(PACK)]
        filled_by_step = [0, 4, 8, 10, 12, 14, 16]
        vector_before = {2: [(quant_v, 1, 0)], 3: [(quant_v, 1, 1)], 7: [(quant_v, 2, 1)]}
        vector_after = {0: [(scale_a, 1, 1), (quant_w, 2, 0, 0, 4), (quant_a, 1, 1)],
                        1: [(quant_w, 2, 1, 0, 4)], 5: [(quant_v, 2, 0)]}

        def v_banks(step, k):
            if not 0 <= k < len(filled_by_step) - 1:
                return [], []
            due = [(step, *key) for key in later_v[filled_by_step[k]:filled_by_step[k + 1]]]
            return due[:2], due[2:]

        last = PAIRS - 1
        for k in range(last):
            vector_order.extend(vector_before.get(k, []) + [(affine, k, e) for e in range(2)])
            if k >= 1:
                vector_order.append((finish, k - 1, 0, 2))
            vector_order.extend(vector_after.get(k, []))
            if k - 2 in ROUND_ON_VECTOR:
                vector_order.append((round_y, k - 2, on_vector, 0, 2))
            if k >= 4 and k % 2 == 1:
                vector_order.append((emit_planes, *place_of(k - 4)[:2]))

            early, late = v_banks(drain_v, k - 1)
            scalar_order.extend(late or early)
            scalar_order.append((squash, k, 0, 2))
            if k >= 2 and k - 2 not in ROUND_ON_VECTOR:
                scalar_order.append((round_y, k - 2, on_scalar, 0, 2))
            early, late = v_banks(drain_v, k)
            if late:
                scalar_order.extend(early)
            if k >= 3:
                scalar_order.append((drain_y, k - 3, 0, 2))

            early, late = v_banks(project, k)
            tensor_order.extend([(mix, k + 1, 0)] + early + [(mix, k + 1, 1)])
            if k >= 3:
                tensor_order.append((turn_y, k - 3, 0, 2))
            tensor_order.extend(late)

        tiles = [(e, e + 1) for e in range(2)]
        vector_order.extend(
            [(affine, last, e) for e in range(2)]
            + [(finish, last - 1, 0, 2), (emit_planes, *place_of(last - 4)[:2]), (round_y, last - 1, on_vector, 0, 2)]
            + [(finish, last, *r) for r in tiles] + [(round_y, last, on_vector, *r) for r in tiles]
            + [(emit_planes, OG - 1, gi) for gi in range(NG)])
        turns = [(last - 3, 0, 2), (last - 1, 0, 2), (last - 2, 0, 2)] + [(last, *r) for r in tiles]
        scalar_order.extend([(squash, last, *r) for r in tiles] + [(round_y, last - 2, on_scalar, 0, 2)]
                            + [(drain_y, *key) for key in turns])
        tensor_order.extend([(turn_y, *key) for key in turns])


        def parts(step, key, lo, hi):
            return [(step, *key, e) for e in range(lo, hi)]

        needs = {
            turn_z: lambda g, h: [],
            turn_x: lambda g, t: [],
            weave_w: lambda og, c, copy, lo, hi: [],
            drain_z: lambda g, h: [(turn_z, g, h)],
            drain_x: lambda g, t: [(turn_x, g, t)],
            scale_z: lambda g, lo, hi: parts(drain_z, [g], lo, hi),
            quant_z: lambda g, lo, hi: parts(drain_z, [g], lo, hi),
            quant_zr: lambda g, lo, hi: parts(scale_z, [g], lo, hi),
            quant_x: lambda g: quarters(drain_x, g),
            quant_w: lambda og, c, lo, hi: parts(weave_w, [og, c], lo, hi),
            scores: lambda gj, gi, s: parts(quant_zr, [gj], 0, 2) + [(quant_z, gi, s // 2)],
            sigmoid: lambda gj, gi, s: [(scores, gj, gi, s)],
            scale_a: lambda gj, gi: quarters(sigmoid, gj, gi),
            quant_a: lambda gj, gi: [(scale_a, gj, gi)],
            project: lambda og, gj, s: [(quant_x, gj)] + [(quant_w, og, c, s) for c in range(FG)],
            drain_v: lambda og, gj, s: [(project, og, gj, s)],
            quant_v: lambda og, gj: quarters(drain_v, og, gj),
            mix: lambda k, e: ([(quant_a, gj, place_of(k)[1]) for gj in range(NG)]
                               + [(quant_v, place_of(k)[0], gj) for gj in range(NG)]),
            affine: lambda k, e: [(mix, k, e)],
            squash: lambda k, lo, hi: parts(affine, [k], lo, hi),
            finish: lambda k, lo, hi: parts(squash, [k], lo, hi),
            round_y: lambda k, copy, lo, hi: parts(finish, [k], lo, hi),
            turn_y: lambda k, lo, hi: parts(round_y, [k], lo, hi),
            drain_y: lambda k, lo, hi: parts(turn_y, [k], lo, hi),
            emit_planes: lambda og, gi: [(drain_y, 2 * (NG * og + gi) + h, e) for h in range(2) for e in range(2)],
        }
        ranged = {scale_z: 1, quant_z: 1, quant_zr: 1, weave_w: 2, quant_w: 2,
                  squash: 1, finish: 1, round_y: 1, turn_y: 1, drain_y: 1}
        fills = {turn_z: "wide", turn_x: "wide", mix: "wide", scores: "quad", project: "quad", turn_y: "quad"}
        empties = {drain_z: "wide", drain_x: "wide", affine: "wide", sigmoid: "quad", drain_v: "quad", drain_y: "quad"}
        free = dict(BANKS)
        done = set()
        orders = [vector_order, scalar_order, tensor_order]
        written = [0, 0, 0]
        while any(written[q] < len(order) for q, order in enumerate(orders)):
            before = sum(written)
            for q, order in enumerate(orders):
                if written[q] == len(order):
                    continue
                step, key = order[written[q]][0], order[written[q]][1:]
                if any(n not in done for n in needs[step](*key)) or (step in fills and free[fills[step]] == 0):
                    continue
                step(*key)
                for part in parts(step, key[:ranged[step]], *key[-2:]) if step in ranged else [(step, *key)]:
                    done.add(part)
                if step in fills:
                    free[fills[step]] = free[fills[step]] - 1
                if step in empties:
                    free[empties[step]] = free[empties[step]] + 1
                written[q] = written[q] + 1
            assert sum(written) > before
